import numpy as np
import ml_dtypes


def mxq(x, axis, fmt="e4m3"):
    dtype, down = {"e4m3": (ml_dtypes.float8_e4m3fn, 7), "e5m2": (ml_dtypes.float8_e5m2, 14)}[fmt]
    v = np.moveaxis(np.asarray(x, np.float32).astype(ml_dtypes.bfloat16).astype(np.float64), axis, -1)
    blocks = v.reshape(v.shape[:-1] + (-1, 32))
    amax = np.abs(blocks).max(-1, keepdims=True)
    byte = np.maximum(np.where(amax > 0, np.frexp(amax)[1] - 1 + 127, 0) - down, 1)
    scale = np.exp2(byte - 127.0)
    codes = (blocks / scale).astype(np.float32).astype(dtype).astype(np.float64)
    return np.moveaxis((codes * scale).reshape(v.shape), -1, axis)


WIDE = False


def mx_kscale(k):
    if not WIDE:
        return np.ones(k)
    levels = np.array([10, -10, 5, -5, 0])
    if k % 512:
        return np.exp2(np.random.permutation(np.resize(levels, k // 32))).repeat(32)
    a = np.empty((k // 512, 16))
    for p in range(k // 512):
        a[p, :8] = np.random.permutation(np.resize(levels, 8))
        for g in range(8):
            far = levels[np.abs(levels - a[p, g]) >= 10]
            a[p, g + 8] = far[np.random.randint(len(far))]
    return np.exp2(a.ravel()).repeat(32)


def f64(x):
    return np.asarray(x).astype(np.float64)


def striped(idx):
    return np.tile(np.asarray(idx).reshape(-1, 16).T, (8, 1)).astype(np.uint16)


def unstriped(offs):
    return offs[:16].T.reshape(-1).astype(np.int64)


E2M1 = np.array([0.0, 0.5, 1.0, 1.5, 2.0, 3.0, 4.0, 6.0, -0.0, -0.5, -1.0, -1.5, -2.0, -3.0, -4.0, -6.0])


def pack_weight(w, fmt):
    k, n = w.shape
    w = f64(np.asarray(w, np.float32).astype(ml_dtypes.bfloat16)).reshape(k // 32, 32, n)
    amax = np.abs(w).max(1)
    if fmt == "e4m3":
        byte = np.frexp(amax)[1] - 1 + 127 - 7
    else:
        mant, ex = np.frexp(amax / 6.0)
        byte = np.where(mant > 0.5, ex, ex - 1) + 127
    byte = np.clip(np.where(amax > 0, byte, 1), 1, 254)
    scaled = (w * np.exp2(127.0 - byte)[:, None, :]).reshape(k, n).astype(np.float32)
    by_word = np.ascontiguousarray(scaled.reshape(k // 512, 128, 4, n).transpose(0, 1, 3, 2))
    if fmt == "e4m3":
        words = by_word.astype(ml_dtypes.float8_e4m3fn).view(np.uint8)
    else:
        c = by_word.astype(ml_dtypes.float4_e2m1fn).view(np.uint8) & 0xF
        words = (c[..., 0::2] | (c[..., 1::2] << 4)).reshape(k // 512, 128, 2 * n)
    return np.ascontiguousarray(words), np.ascontiguousarray(byte.astype(np.uint8).reshape(k // 512, 16, n))


def unpack_weight(words, scales, fmt):
    g, _, n = scales.shape
    words = np.ascontiguousarray(words).reshape(g, 128, n, -1)
    if fmt == "e4m3":
        vals = words.view(ml_dtypes.float8_e4m3fn).astype(np.float64)
    else:
        nib = np.empty((g, 128, n, 4), np.uint8)
        nib[..., 0::2] = words & 0xF
        nib[..., 1::2] = words >> 4
        vals = E2M1[nib]
    vals = vals * np.repeat(np.exp2(scales.astype(np.float64) - 127.0), 8, axis=1)[..., None]
    return vals.transpose(0, 1, 3, 2).reshape(g * 512, n)


def bf(x):
    return np.asarray(x, np.float32).astype(ml_dtypes.bfloat16)


def planes(Y):
    r, m = Y.shape
    b = f64(bf(Y)).reshape(r // 32, 32, m)
    amax = np.abs(b).max(1)
    byte = np.clip(np.where(amax > 0, np.frexp(amax)[1] - 1 + 127 - 7, 1), 1, 254)
    codes = (b * np.exp2(127.0 - byte)[:, None, :]).reshape(r, m).astype(np.float32).astype(ml_dtypes.float8_e4m3fn).view(np.uint8)
    words = codes.reshape(r // 512, 128, 4, m).transpose(0, 1, 3, 2)
    return np.ascontiguousarray(words), np.ascontiguousarray(byte.astype(np.uint8).reshape(r // 512, 16, m))


B, N, T, D, NQ = 1, 512, 2048, 512, 512


def setup_inputs():
    n = np.random.standard_normal
    idx = np.random.permutation(T)[:B * N]
    s = mx_kscale(D)[:, None]
    kp = pack_weight(n((D, T)) / s, "e4m3")
    return {
        "qT": (n((B, D, NQ)) * s * (0.50 / np.sqrt(D))).astype(np.float32),
        "k_words": kp[0],
        "k_scales": kp[1],
        "kn": np.tile(np.random.uniform(1.0, 4.0, 2048), (128, 1)).astype(np.float32),
        "qn": (np.random.uniform(1.0, 4.0, (B, NQ, 1))).astype(np.float32),
        "offs": striped(idx),
    }


def reference(qT, k_words, k_scales, kn, qn, offs):
    idx = unstriped(offs)
    pick = lambda x, which: x[:, which].reshape(x.shape[0], B, -1).transpose(1, 0, 2)
    k = unpack_weight(k_words, k_scales, "e4m3")
    kg = pick(k, idx)
    qq = mxq(f64(qT), 1, "e4m3")
    a = qq.transpose(0, 2, 1) @ kg
    t = 1.0 / (1.0 + np.maximum(f64(qn) + pick(f64(kn), idx)[:, :1, :] - 2.0 * a, 0.0))
    y = t / np.sum(t, axis=-1, keepdims=True)
    Y = y[0]
    words, scales = planes(Y)
    return Y, words, scales

@@ -1,0 +1,165 @@
+from contextlib import ExitStack
+
+import concourse.mybir as mybir
+from concourse.masks import make_identity
+
+D, NQ, T, N = 512, 512, 2048, 512
+FLOPS = 2 * D * NQ * N
+
+F32 = mybir.dt.float32
+BF16 = mybir.dt.bfloat16
+I32 = mybir.dt.int32
+U32 = mybir.dt.uint32
+U16 = mybir.dt.uint16
+U8 = mybir.dt.uint8
+FP8X4 = mybir.dt.float8_e4m3fn_x4
+ALU = mybir.AluOpType
+ACT = mybir.ActivationFunctionType
+
+P = 128
+PACK = 4
+HALF = N // 2
+
+
+def tile_attend_plq_assign_topk_kernel(tc, qT, k_words, k_scales, kn, qn, offs, out_0, out_1, out_2):
+    nc = tc.nc
+    with ExitStack() as ctx:
+        sb = ctx.enter_context(tc.tile_pool(name="sb", bufs=1))
+        ps = ctx.enter_context(tc.psum_pool(name="ps", bufs=1))
+
+        offsets = sb.tile([P, N // 16], U16, name="offsets")
+        nc.sync.dma_start(offsets[:], offs)
+
+        kn_pool = sb.tile([P, T], F32, name="kn_pool")
+        nc.sync.dma_start(out=kn_pool[P - 1 : P, :], in_=kn[0:1, :])
+        scale_pool = sb.tile([P, T], U8, name="scale_pool")
+        nc.vector.memset(scale_pool[:].bitcast(I32), 0)
+        nc.vector.memset(kn_pool[0 : P - 1, :], 0.0)
+        q_raw = sb.tile([P, PACK, NQ], F32, name="q_raw")
+        nc.sync.dma_start(out=q_raw[:], in_=qT[0].rearrange("(p j) q -> p j q", j=PACK))
+        for quad in range(4):
+            nc.sync.dma_start(
+                out=scale_pool[32 * quad : 32 * quad + 4, :].bitcast(I32),
+                in_=k_scales[0, 4 * quad : 4 * quad + 4, :].bitcast(I32),
+            )
+        word_pool = sb.tile([P, T], I32, name="word_pool")
+        nc.sync.dma_start(out=word_pool[:], in_=k_words[0].rearrange("p t r -> p (t r)").bitcast(I32))
+        qn_cols = sb.tile([P, PACK], F32, name="qn_cols")
+        nc.sync.dma_start(out=qn_cols[:], in_=qn[0].rearrange("(p t) o -> p (t o)", t=PACK))
+
+        ident = sb.tile([P, P], F32, name="ident")
+        make_identity(nc, ident[:])
+        warm = sb.tile([P, 1], F32, name="warm")
+        nc.scalar.activation(warm[:], ident[:, 0:1], ACT.Abs_reciprocal_sqrt, bias=1.0)
+
+        kn_row = sb.tile([P, N], F32, name="kn_row")
+        nc.vector.tensor_copy(kn_row[:], kn_pool[:].indirect(offsets[:]))
+        kn_turned = ps.tile([P, PACK, P], F32, name="kn_turned", tag="turned")
+        for j in range(PACK):
+            nc.tensor.transpose(kn_turned[:, j, :], kn_row[:, j * P : (j + 1) * P], ident[:])
+        kn_cols = sb.tile([P, PACK], F32, name="kn_cols")
+        nc.scalar.copy(kn_cols[:], kn_turned[:, :, P - 1])
+        kn_spread = ps.tile([P, N], F32, name="kn_spread", tag="spread")
+        for j in range(PACK):
+            nc.tensor.transpose(kn_spread[:, j * P : (j + 1) * P], kn_cols[:, j : j + 1].to_broadcast([P, P]), ident[:])
+        kn_all = sb.tile([P, N], F32, name="kn_all")
+        nc.scalar.copy(kn_all[:], kn_spread[:])
+
+        k_scale = sb.tile([P, N], U8, name="k_scale", align_bytes=64)
+        nc.vector.tensor_copy(k_scale[:], scale_pool[:].indirect(offsets[:]))
+
+        q_bf = sb.tile([P, PACK, P, PACK], BF16, name="q_bf", align_bytes=64)
+        nc.scalar.copy(q_bf[:].rearrange("p t m j -> p m j t"), q_raw[:].rearrange("p j (m t) -> p m j t", t=PACK))
+        q_code = sb.tile([P, NQ], U32, name="q_code", align_bytes=64)
+        q_scale = sb.tile([P, NQ], U8, name="q_scale", align_bytes=64)
+        nc.vector.quantize_mx(out=q_code[:].bitcast(FP8X4), scales=q_scale[:], in_=q_bf[:].rearrange("p t m j -> p (t m j)"))
+
+        k_code = [sb.tile([P, HALF], U32, name="k_code%d" % h, align_bytes=64) for h in range(2)]
+        for h in range(2):
+            nc.vector.tensor_copy(k_code[h][:], word_pool[:].bitcast(U32).indirect(offsets[:, 16 * h : 16 * (h + 1)]))
+
+        tags = {(0, 3): "turned", (1, 3): "spread"}
+        banks = {
+            (h, t): ps.tile([P, HALF], F32, name="bank%d%d" % (h, t), tag=tags.get((h, t), "bank%d%d" % (h, t)))
+            for h in range(2)
+            for t in range(PACK)
+        }
+        for h in range(2):
+            for t in range(PACK):
+                nc.tensor.matmul_mx(
+                    out=banks[h, t][:],
+                    lhsT=q_code[:, t * P : (t + 1) * P].bitcast(FP8X4),
+                    lhsT_scale=q_scale[:, t * P : (t + 1) * P],
+                    rhs=k_code[h][:].bitcast(FP8X4),
+                    rhs_scale=k_scale[:, h * HALF : (h + 1) * HALF],
+                    start=True,
+                    stop=True,
+                )
+
+        y = sb.tile([P, PACK, N], F32, name="y")
+        out_rows = out_0.rearrange("(p t) i -> p t i", t=PACK)
+        dist = [sb.tile([P, N], F32, name="dist%d" % t) for t in range(PACK)]
+        root = [sb.tile([P, N], F32, name="root%d" % t) for t in range(PACK)]
+        wt = [sb.tile([P, N], F32, name="wt%d" % t) for t in range(PACK)]
+        total = [sb.tile([P, 1], F32, name="total%d" % t) for t in range(PACK)]
+        inv = [sb.tile([P, 1], F32, name="inv%d" % t) for t in range(PACK)]
+        halves = [slice(0, HALF), slice(HALF, N)]
+
+        def distances(t):
+            for h in range(2):
+                nc.vector.scalar_tensor_tensor(dist[t][:, halves[h]], banks[h, t][:], -2.0, kn_all[:, halves[h]], ALU.mult, ALU.add)
+            for h in range(2):
+                nc.vector.tensor_scalar(dist[t][:, halves[h]], dist[t][:, halves[h]], qn_cols[:, t : t + 1], 0.0, ALU.add, ALU.max)
+
+        def roots(t, cols):
+            nc.scalar.activation(root[t][:, cols], dist[t][:, cols], ACT.Abs_reciprocal_sqrt, bias=1.0)
+
+        def squares(t):
+            nc.scalar.activation(wt[t][:], root[t][:], ACT.Square, accum_out=total[t][:])
+
+        def squares_on_vector(t):
+            nc.vector.scalar_tensor_tensor(wt[t][:], root[t][:], 1.0, root[t][:], ALU.mult, ALU.mult, accum_out=total[t][:])
+
+        def back(t):
+            nc.vector.reciprocal(inv[t][:], total[t][:])
+            nc.vector.tensor_scalar(y[:, t, :], wt[t][:], inv[t][:], None, ALU.mult)
+            nc.sync.dma_start(out=out_rows[:, t, :], in_=y[:, t, :])
+
+        for t in range(PACK):
+            distances(t)
+        roots(0, halves[0])
+        roots(0, halves[1])
+        squares(0)
+        roots(1, slice(0, N))
+        roots(2, slice(0, N))
+        squares_on_vector(1)
+        roots(3, slice(0, N))
+        squares(2)
+        squares(3)
+        for t in range(PACK):
+            back(t)
+
+        y_code = sb.tile([P, N], U32, name="y_code", align_bytes=64)
+        y_scale = sb.tile([P, N], U8, name="y_scale", align_bytes=64)
+        out_words = out_1[0].rearrange("p i u -> p (i u)").bitcast(I32)
+        y_bf = [sb.tile([P, P, PACK], BF16, name="y_bf%d" % c, align_bytes=64) for c in range(4)]
+        for c in (0, 2, 1, 3):
+            cols = slice(c * P, (c + 1) * P)
+            dst = y_bf[c][:].rearrange("p (c i) t -> p c t i", i=4)
+            src = y[:, :, cols].rearrange("p t (c i) -> p c t i", i=4)
+            if c < 2:
+                nc.vector.tensor_copy(dst, src)
+            else:
+                nc.scalar.copy(dst, src)
+        for c in range(4):
+            cols = slice(c * P, (c + 1) * P)
+            nc.vector.quantize_mx(out=y_code[:, cols].bitcast(FP8X4), scales=y_scale[:, cols], in_=y_bf[c][:].rearrange("p i t -> p (i t)"))
+            if c % 2 == 1:
+                pair = slice((c - 1) * P, (c + 1) * P)
+                nc.sync.dma_start(out=out_words[:, pair], in_=y_code[:, pair].bitcast(I32))
+        for quad in range(4):
+            queue = nc.scalar if quad % 2 == 0 else nc.sync
+            queue.dma_start(
+                out=out_2[0, 4 * quad : 4 * quad + 4, :].bitcast(I32),
+                in_=y_scale[32 * quad : 32 * quad + 4, :].bitcast(I32),
+            )

@@ -19,6 +19,7 @@ ACT = mybir.ActivationFunctionType
 P = 128
 PACK = 4
 HALF = N // 2
+Q_SPLIT = 64
 
 
 def tile_attend_plq_assign_topk_kernel(tc, qT, k_words, k_scales, kn, qn, offs, out_0, out_1, out_2):
@@ -32,18 +33,20 @@ def tile_attend_plq_assign_topk_kernel(tc, qT, k_words, k_scales, kn, qn, offs, 
 
         kn_pool = sb.tile([P, T], F32, name="kn_pool")
         nc.sync.dma_start(out=kn_pool[P - 1 : P, :], in_=kn[0:1, :])
-        scale_pool = sb.tile([P, T], U8, name="scale_pool")
-        nc.vector.memset(scale_pool[:].bitcast(I32), 0)
         nc.vector.memset(kn_pool[0 : P - 1, :], 0.0)
-        q_raw = sb.tile([P, PACK, NQ], F32, name="q_raw")
-        nc.sync.dma_start(out=q_raw[:], in_=qT[0].rearrange("(p j) q -> p j q", j=PACK))
+        scale_pool = sb.tile([P, T], U8, name="scale_pool")
+        nc.gpsimd.memset(scale_pool[:].bitcast(I32), 0)
         for quad in range(4):
             nc.sync.dma_start(
                 out=scale_pool[32 * quad : 32 * quad + 4, :].bitcast(I32),
                 in_=k_scales[0, 4 * quad : 4 * quad + 4, :].bitcast(I32),
             )
+
+        q_raw = sb.tile([P, PACK, NQ], F32, name="q_raw")
+        nc.sync.dma_start(out=q_raw[:], in_=qT[0].rearrange("(p j) q -> p j q", j=PACK))
         word_pool = sb.tile([P, T], I32, name="word_pool")
         nc.sync.dma_start(out=word_pool[:], in_=k_words[0].rearrange("p t r -> p (t r)").bitcast(I32))
+
         qn_cols = sb.tile([P, PACK], F32, name="qn_cols")
         nc.sync.dma_start(out=qn_cols[:], in_=qn[0].rearrange("(p t) o -> p (t o)", t=PACK))
 
@@ -69,7 +72,10 @@ def tile_attend_plq_assign_topk_kernel(tc, qT, k_words, k_scales, kn, qn, offs, 
         nc.vector.tensor_copy(k_scale[:], scale_pool[:].indirect(offsets[:]))
 
         q_bf = sb.tile([P, PACK, P, PACK], BF16, name="q_bf", align_bytes=64)
-        nc.scalar.copy(q_bf[:].rearrange("p t m j -> p m j t"), q_raw[:].rearrange("p j (m t) -> p m j t", t=PACK))
+        q_dst = q_bf[:].rearrange("p t m j -> p m j t")
+        q_src = q_raw[:].rearrange("p j (m t) -> p m j t", t=PACK)
+        nc.scalar.copy(q_dst[:, 0:Q_SPLIT], q_src[:, 0:Q_SPLIT])
+        nc.vector.tensor_copy(q_dst[:, Q_SPLIT:P], q_src[:, Q_SPLIT:P])
         q_code = sb.tile([P, NQ], U32, name="q_code", align_bytes=64)
         q_scale = sb.tile([P, NQ], U8, name="q_scale", align_bytes=64)
         nc.vector.quantize_mx(out=q_code[:].bitcast(FP8X4), scales=q_scale[:], in_=q_bf[:].rearrange("p t m j -> p (t m j)"))
@@ -122,7 +128,8 @@ def tile_attend_plq_assign_topk_kernel(tc, qT, k_words, k_scales, kn, qn, offs, 
 
         def back(t):
             nc.vector.reciprocal(inv[t][:], total[t][:])
-            nc.vector.tensor_scalar(y[:, t, :], wt[t][:], inv[t][:], None, ALU.mult)
+            for cols in ([slice(0, N)] if t < PACK - 1 else [halves[1], halves[0]]):
+                nc.vector.tensor_scalar(y[:, t, cols], wt[t][:, cols], inv[t][:], None, ALU.mult)
             nc.sync.dma_start(out=out_rows[:, t, :], in_=y[:, t, :])
 
         for t in range(PACK):

@@ -31,6 +31,8 @@ def tile_attend_plq_assign_topk_kernel(tc, qT, k_words, k_scales, kn, qn, offs, 
         offsets = sb.tile([P, N // 16], U16, name="offsets")
         nc.sync.dma_start(offsets[:], offs)
 
+        one = sb.tile([P, 1], F32, name="one")
+        nc.vector.memset(one[:], 1.0)
         kn_pool = sb.tile([P, T], F32, name="kn_pool")
         nc.sync.dma_start(out=kn_pool[P - 1 : P, :], in_=kn[0:1, :])
         nc.vector.memset(kn_pool[0 : P - 1, :], 0.0)
@@ -53,16 +55,16 @@ def tile_attend_plq_assign_topk_kernel(tc, qT, k_words, k_scales, kn, qn, offs, 
         ident = sb.tile([P, P], F32, name="ident")
         make_identity(nc, ident[:])
         warm = sb.tile([P, 1], F32, name="warm")
-        nc.scalar.activation(warm[:], ident[:, 0:1], ACT.Abs_reciprocal_sqrt, bias=1.0)
+        nc.scalar.activation(warm[:], one[:], ACT.Abs_reciprocal_sqrt, bias=one[:])
 
         kn_row = sb.tile([P, N], F32, name="kn_row")
         nc.vector.tensor_copy(kn_row[:], kn_pool[:].indirect(offsets[:]))
-        kn_turned = ps.tile([P, PACK, P], F32, name="kn_turned", tag="turned")
+        kn_turned = ps.tile([P, PACK, P], F32, name="kn_turned")
         for j in range(PACK):
             nc.tensor.transpose(kn_turned[:, j, :], kn_row[:, j * P : (j + 1) * P], ident[:])
         kn_cols = sb.tile([P, PACK], F32, name="kn_cols")
         nc.scalar.copy(kn_cols[:], kn_turned[:, :, P - 1])
-        kn_spread = ps.tile([P, N], F32, name="kn_spread", tag="spread")
+        kn_spread = ps.tile([P, N], F32, name="kn_spread")
         for j in range(PACK):
             nc.tensor.transpose(kn_spread[:, j * P : (j + 1) * P], kn_cols[:, j : j + 1].to_broadcast([P, P]), ident[:])
         kn_all = sb.tile([P, N], F32, name="kn_all")
@@ -80,27 +82,23 @@ def tile_attend_plq_assign_topk_kernel(tc, qT, k_words, k_scales, kn, qn, offs, 
         q_scale = sb.tile([P, NQ], U8, name="q_scale", align_bytes=64)
         nc.vector.quantize_mx(out=q_code[:].bitcast(FP8X4), scales=q_scale[:], in_=q_bf[:].rearrange("p t m j -> p (t m j)"))
 
-        k_code = [sb.tile([P, HALF], U32, name="k_code%d" % h, align_bytes=64) for h in range(2)]
+        k_code = sb.tile([P, N], U32, name="k_code", align_bytes=64)
+        halves = [slice(0, HALF), slice(HALF, N)]
         for h in range(2):
-            nc.vector.tensor_copy(k_code[h][:], word_pool[:].bitcast(U32).indirect(offsets[:, 16 * h : 16 * (h + 1)]))
+            nc.vector.tensor_copy(k_code[:, halves[h]], word_pool[:].bitcast(U32).indirect(offsets[:, 16 * h : 16 * (h + 1)]))
 
-        tags = {(0, 3): "turned", (1, 3): "spread"}
-        banks = {
-            (h, t): ps.tile([P, HALF], F32, name="bank%d%d" % (h, t), tag=tags.get((h, t), "bank%d%d" % (h, t)))
-            for h in range(2)
-            for t in range(PACK)
-        }
-        for h in range(2):
-            for t in range(PACK):
-                nc.tensor.matmul_mx(
-                    out=banks[h, t][:],
-                    lhsT=q_code[:, t * P : (t + 1) * P].bitcast(FP8X4),
-                    lhsT_scale=q_scale[:, t * P : (t + 1) * P],
-                    rhs=k_code[h][:].bitcast(FP8X4),
-                    rhs_scale=k_scale[:, h * HALF : (h + 1) * HALF],
-                    start=True,
-                    stop=True,
-                )
+        pieces = [(t, cols) for cols in halves for t in range(2)] + [(t, slice(0, N)) for t in range(2, PACK)]
+        banks = [ps.tile([P, cols.stop - cols.start], F32, name="bank%d" % b) for b, (t, cols) in enumerate(pieces)]
+        for bank, (t, cols) in zip(banks, pieces):
+            nc.tensor.matmul_mx(
+                out=bank[:],
+                lhsT=q_code[:, t * P : (t + 1) * P].bitcast(FP8X4),
+                lhsT_scale=q_scale[:, t * P : (t + 1) * P],
+                rhs=k_code[:, cols].bitcast(FP8X4),
+                rhs_scale=k_scale[:, cols],
+                start=True,
+                stop=True,
+            )
 
         y = sb.tile([P, PACK, N], F32, name="y")
         out_rows = out_0.rearrange("(p t) i -> p t i", t=PACK)
@@ -109,16 +107,17 @@ def tile_attend_plq_assign_topk_kernel(tc, qT, k_words, k_scales, kn, qn, offs, 
         wt = [sb.tile([P, N], F32, name="wt%d" % t) for t in range(PACK)]
         total = [sb.tile([P, 1], F32, name="total%d" % t) for t in range(PACK)]
         inv = [sb.tile([P, 1], F32, name="inv%d" % t) for t in range(PACK)]
-        halves = [slice(0, HALF), slice(HALF, N)]
 
-        def distances(t):
-            for h in range(2):
-                nc.vector.scalar_tensor_tensor(dist[t][:, halves[h]], banks[h, t][:], -2.0, kn_all[:, halves[h]], ALU.mult, ALU.add)
-            for h in range(2):
-                nc.vector.tensor_scalar(dist[t][:, halves[h]], dist[t][:, halves[h]], qn_cols[:, t : t + 1], 0.0, ALU.add, ALU.max)
+        def cross(b):
+            t, cols = pieces[b]
+            nc.vector.scalar_tensor_tensor(dist[t][:, cols], banks[b][:], -2.0, kn_all[:, cols], ALU.mult, ALU.add)
+
+        def clamp(b):
+            t, cols = pieces[b]
+            nc.vector.tensor_scalar(dist[t][:, cols], dist[t][:, cols], qn_cols[:, t : t + 1], 0.0, ALU.add, ALU.max)
 
         def roots(t, cols):
-            nc.scalar.activation(root[t][:, cols], dist[t][:, cols], ACT.Abs_reciprocal_sqrt, bias=1.0)
+            nc.scalar.activation(root[t][:, cols], dist[t][:, cols], ACT.Abs_reciprocal_sqrt, bias=one[:])
 
         def squares(t):
             nc.scalar.activation(wt[t][:], root[t][:], ACT.Square, accum_out=total[t][:])
@@ -128,20 +127,25 @@ def tile_attend_plq_assign_topk_kernel(tc, qT, k_words, k_scales, kn, qn, offs, 
 
         def back(t):
             nc.vector.reciprocal(inv[t][:], total[t][:])
-            for cols in ([slice(0, N)] if t < PACK - 1 else [halves[1], halves[0]]):
-                nc.vector.tensor_scalar(y[:, t, cols], wt[t][:, cols], inv[t][:], None, ALU.mult)
+            if t < PACK - 1:
+                nc.vector.tensor_scalar(y[:, t, :], wt[t][:], inv[t][:], None, ALU.mult)
+            else:
+                nc.scalar.activation(y[:, t, halves[1]], wt[t][:, halves[1]], ACT.Copy, scale=inv[t][:])
+                nc.vector.tensor_scalar(y[:, t, halves[0]], wt[t][:, halves[0]], inv[t][:], None, ALU.mult)
             nc.sync.dma_start(out=out_rows[:, t, :], in_=y[:, t, :])
 
-        for t in range(PACK):
-            distances(t)
-        roots(0, halves[0])
-        roots(0, halves[1])
+        for b in range(0, len(pieces), 2):
+            cross(b)
+            cross(b + 1)
+            clamp(b)
+            clamp(b + 1)
+        for t, cols in pieces[0:4]:
+            roots(t, cols)
         squares(0)
-        roots(1, slice(0, N))
+        squares(1)
         roots(2, slice(0, N))
-        squares_on_vector(1)
         roots(3, slice(0, N))
-        squares(2)
+        squares_on_vector(2)
         squares(3)
         for t in range(PACK):
             back(t)
@@ -149,21 +153,20 @@ def tile_attend_plq_assign_topk_kernel(tc, qT, k_words, k_scales, kn, qn, offs, 
         y_code = sb.tile([P, N], U32, name="y_code", align_bytes=64)
         y_scale = sb.tile([P, N], U8, name="y_scale", align_bytes=64)
         out_words = out_1[0].rearrange("p i u -> p (i u)").bitcast(I32)
-        y_bf = [sb.tile([P, P, PACK], BF16, name="y_bf%d" % c, align_bytes=64) for c in range(4)]
-        for c in (0, 2, 1, 3):
-            cols = slice(c * P, (c + 1) * P)
-            dst = y_bf[c][:].rearrange("p (c i) t -> p c t i", i=4)
+        spans = [slice(0, HALF), slice(HALF, HALF + P), slice(HALF + P, N)]
+        y_bf = [sb.tile([P, c.stop - c.start, PACK], BF16, name="y_bf%d" % c.start, align_bytes=64) for c in spans]
+        for k, cols in enumerate(spans):
+            dst = y_bf[k][:].rearrange("p (c i) t -> p c t i", i=4)
             src = y[:, :, cols].rearrange("p t (c i) -> p c t i", i=4)
-            if c < 2:
+            if k == 0:
                 nc.vector.tensor_copy(dst, src)
             else:
                 nc.scalar.copy(dst, src)
-        for c in range(4):
-            cols = slice(c * P, (c + 1) * P)
-            nc.vector.quantize_mx(out=y_code[:, cols].bitcast(FP8X4), scales=y_scale[:, cols], in_=y_bf[c][:].rearrange("p i t -> p (i t)"))
-            if c % 2 == 1:
-                pair = slice((c - 1) * P, (c + 1) * P)
-                nc.sync.dma_start(out=out_words[:, pair], in_=y_code[:, pair].bitcast(I32))
+        for k in (1, 0, 2):
+            cols = spans[k]
+            nc.vector.quantize_mx(out=y_code[:, cols].bitcast(FP8X4), scales=y_scale[:, cols], in_=y_bf[k][:].rearrange("p i t -> p (i t)"))
+        for cols in halves:
+            nc.sync.dma_start(out=out_words[:, cols], in_=y_code[:, cols].bitcast(I32))
         for quad in range(4):
             queue = nc.scalar if quad % 2 == 0 else nc.sync
             queue.dma_start(

@@ -38,11 +38,8 @@ def tile_attend_plq_assign_topk_kernel(tc, qT, k_words, k_scales, kn, qn, offs, 
         nc.vector.memset(kn_pool[0 : P - 1, :], 0.0)
         scale_pool = sb.tile([P, T], U8, name="scale_pool")
         nc.gpsimd.memset(scale_pool[:].bitcast(I32), 0)
-        for quad in range(4):
-            nc.sync.dma_start(
-                out=scale_pool[32 * quad : 32 * quad + 4, :].bitcast(I32),
-                in_=k_scales[0, 4 * quad : 4 * quad + 4, :].bitcast(I32),
-            )
+        for r in range(4):
+            nc.sync.dma_start(out=scale_pool[r:P:32, :].bitcast(I32), in_=k_scales[0, r:16:4, :].bitcast(I32))
 
         q_raw = sb.tile([P, PACK, NQ], F32, name="q_raw")
         nc.sync.dma_start(out=q_raw[:], in_=qT[0].rearrange("(p j) q -> p j q", j=PACK))
@@ -167,9 +164,6 @@ def tile_attend_plq_assign_topk_kernel(tc, qT, k_words, k_scales, kn, qn, offs, 
             nc.vector.quantize_mx(out=y_code[:, cols].bitcast(FP8X4), scales=y_scale[:, cols], in_=y_bf[k][:].rearrange("p i t -> p (i t)"))
         for cols in halves:
             nc.sync.dma_start(out=out_words[:, cols], in_=y_code[:, cols].bitcast(I32))
-        for quad in range(4):
-            queue = nc.scalar if quad % 2 == 0 else nc.sync
-            queue.dma_start(
-                out=out_2[0, 4 * quad : 4 * quad + 4, :].bitcast(I32),
-                in_=y_scale[32 * quad : 32 * quad + 4, :].bitcast(I32),
-            )
+        for r in range(4):
+            queue = nc.scalar if r % 2 == 0 else nc.sync
+            queue.dma_start(out=out_2[0, r:16:4, :].bitcast(I32), in_=y_scale[r:P:32, :].bitcast(I32))

@@ -20,6 +20,7 @@ P = 128
 PACK = 4
 HALF = N // 2
 Q_SPLIT = 64
+ROWS = 16
 
 
 def tile_attend_plq_assign_topk_kernel(tc, qT, k_words, k_scales, kn, qn, offs, out_0, out_1, out_2):
@@ -33,13 +34,12 @@ def tile_attend_plq_assign_topk_kernel(tc, qT, k_words, k_scales, kn, qn, offs, 
 
         one = sb.tile([P, 1], F32, name="one")
         nc.vector.memset(one[:], 1.0)
+        scale_pool = sb.tile([P, T], U8, name="scale_pool")
+        nc.sync.dma_start(out=scale_pool[P - ROWS : P, :].bitcast(I32), in_=k_scales[0].bitcast(I32))
+        nc.gpsimd.memset(scale_pool[0 : P - ROWS, :].bitcast(I32), 0)
         kn_pool = sb.tile([P, T], F32, name="kn_pool")
         nc.sync.dma_start(out=kn_pool[P - 1 : P, :], in_=kn[0:1, :])
         nc.vector.memset(kn_pool[0 : P - 1, :], 0.0)
-        scale_pool = sb.tile([P, T], U8, name="scale_pool")
-        nc.gpsimd.memset(scale_pool[:].bitcast(I32), 0)
-        for r in range(4):
-            nc.sync.dma_start(out=scale_pool[r:P:32, :].bitcast(I32), in_=k_scales[0, r:16:4, :].bitcast(I32))
 
         q_raw = sb.tile([P, PACK, NQ], F32, name="q_raw")
         nc.sync.dma_start(out=q_raw[:], in_=qT[0].rearrange("(p j) q -> p j q", j=PACK))
@@ -54,6 +54,14 @@ def tile_attend_plq_assign_topk_kernel(tc, qT, k_words, k_scales, kn, qn, offs, 
         warm = sb.tile([P, 1], F32, name="warm")
         nc.scalar.activation(warm[:], one[:], ACT.Abs_reciprocal_sqrt, bias=one[:])
 
+        picked = sb.tile([P, N], U8, name="picked")
+        nc.vector.tensor_copy(picked[:], scale_pool[:].indirect(offsets[:]))
+        k_scale = sb.tile([P, N], U8, name="k_scale", align_bytes=64)
+        nc.gpsimd.memset(k_scale[:].bitcast(I32), 0)
+        for quad in range(4):
+            first = P - ROWS + 4 * quad
+            nc.scalar.dma_start(out=k_scale[32 * quad : 32 * quad + 4, :].bitcast(I32), in_=picked[first : first + 4, :].bitcast(I32))
+
         kn_row = sb.tile([P, N], F32, name="kn_row")
         nc.vector.tensor_copy(kn_row[:], kn_pool[:].indirect(offsets[:]))
         kn_turned = ps.tile([P, PACK, P], F32, name="kn_turned")
@@ -66,9 +74,6 @@ def tile_attend_plq_assign_topk_kernel(tc, qT, k_words, k_scales, kn, qn, offs, 
             nc.tensor.transpose(kn_spread[:, j * P : (j + 1) * P], kn_cols[:, j : j + 1].to_broadcast([P, P]), ident[:])
         kn_all = sb.tile([P, N], F32, name="kn_all")
         nc.scalar.copy(kn_all[:], kn_spread[:])
-
-        k_scale = sb.tile([P, N], U8, name="k_scale", align_bytes=64)
-        nc.vector.tensor_copy(k_scale[:], scale_pool[:].indirect(offsets[:]))
 
         q_bf = sb.tile([P, PACK, P, PACK], BF16, name="q_bf", align_bytes=64)
         q_dst = q_bf[:].rearrange("p t m j -> p m j t")

@@ -20,7 +20,9 @@ P = 128
 PACK = 4
 HALF = N // 2
 Q_SPLIT = 64
+LOWEST = -3.0e38
 ROWS = 16
+TAIL = 320
 
 
 def tile_attend_plq_assign_topk_kernel(tc, qT, k_words, k_scales, kn, qn, offs, out_0, out_1, out_2):
@@ -73,7 +75,9 @@ def tile_attend_plq_assign_topk_kernel(tc, qT, k_words, k_scales, kn, qn, offs, 
         for j in range(PACK):
             nc.tensor.transpose(kn_spread[:, j * P : (j + 1) * P], kn_cols[:, j : j + 1].to_broadcast([P, P]), ident[:])
         kn_all = sb.tile([P, N], F32, name="kn_all")
-        nc.scalar.copy(kn_all[:], kn_spread[:])
+        nc.scalar.activation(kn_all[:], kn_spread[:], ACT.Copy, scale=0.5)
+        qn_half = sb.tile([P, PACK], F32, name="qn_half")
+        nc.scalar.activation(qn_half[:], qn_cols[:], ACT.Copy, scale=0.5)
 
         q_bf = sb.tile([P, PACK, P, PACK], BF16, name="q_bf", align_bytes=64)
         q_dst = q_bf[:].rearrange("p t m j -> p m j t")
@@ -112,14 +116,15 @@ def tile_attend_plq_assign_topk_kernel(tc, qT, k_words, k_scales, kn, qn, offs, 
 
         def cross(b):
             t, cols = pieces[b]
-            nc.vector.scalar_tensor_tensor(dist[t][:, cols], banks[b][:], -2.0, kn_all[:, cols], ALU.mult, ALU.add)
+            nc.vector.scalar_tensor_tensor(dist[t][:, cols], banks[b][:], qn_half[:, t : t + 1], kn_all[:, cols], ALU.subtract, ALU.subtract)
 
         def clamp(b):
             t, cols = pieces[b]
-            nc.vector.tensor_scalar(dist[t][:, cols], dist[t][:, cols], qn_cols[:, t : t + 1], 0.0, ALU.add, ALU.max)
+            engine = nc.gpsimd if 2 <= b <= 4 else nc.vector
+            engine.tensor_scalar(dist[t][:, cols], dist[t][:, cols], 0.0, LOWEST, ALU.min, ALU.max)
 
         def roots(t, cols):
-            nc.scalar.activation(root[t][:, cols], dist[t][:, cols], ACT.Abs_reciprocal_sqrt, bias=one[:])
+            nc.scalar.activation(root[t][:, cols], dist[t][:, cols], ACT.Abs_reciprocal_sqrt, bias=one[:], scale=-2.0)
 
         def squares(t):
             nc.scalar.activation(wt[t][:], root[t][:], ACT.Square, accum_out=total[t][:])
@@ -132,8 +137,8 @@ def tile_attend_plq_assign_topk_kernel(tc, qT, k_words, k_scales, kn, qn, offs, 
             if t < PACK - 1:
                 nc.vector.tensor_scalar(y[:, t, :], wt[t][:], inv[t][:], None, ALU.mult)
             else:
-                nc.scalar.activation(y[:, t, halves[1]], wt[t][:, halves[1]], ACT.Copy, scale=inv[t][:])
-                nc.vector.tensor_scalar(y[:, t, halves[0]], wt[t][:, halves[0]], inv[t][:], None, ALU.mult)
+                nc.scalar.activation(y[:, t, TAIL:N], wt[t][:, TAIL:N], ACT.Copy, scale=inv[t][:])
+                nc.vector.tensor_scalar(y[:, t, 0:TAIL], wt[t][:, 0:TAIL], inv[t][:], None, ALU.mult)
             nc.sync.dma_start(out=out_rows[:, t, :], in_=y[:, t, :])
 
         for b in range(0, len(pieces), 2):
@@ -144,18 +149,19 @@ def tile_attend_plq_assign_topk_kernel(tc, qT, k_words, k_scales, kn, qn, offs, 
         for t, cols in pieces[0:4]:
             roots(t, cols)
         squares(0)
-        squares(1)
         roots(2, slice(0, N))
         roots(3, slice(0, N))
+        squares_on_vector(1)
+        back(0)
         squares_on_vector(2)
         squares(3)
-        for t in range(PACK):
+        for t in range(1, PACK):
             back(t)
 
         y_code = sb.tile([P, N], U32, name="y_code", align_bytes=64)
         y_scale = sb.tile([P, N], U8, name="y_scale", align_bytes=64)
         out_words = out_1[0].rearrange("p i u -> p (i u)").bitcast(I32)
-        spans = [slice(0, HALF), slice(HALF, HALF + P), slice(HALF + P, N)]
+        spans = [slice(0, TAIL), slice(TAIL, TAIL + P), slice(TAIL + P, N)]
         y_bf = [sb.tile([P, c.stop - c.start, PACK], BF16, name="y_bf%d" % c.start, align_bytes=64) for c in spans]
         for k, cols in enumerate(spans):
             dst = y_bf[k][:].rearrange("p (c i) t -> p c t i", i=4)
@@ -164,9 +170,13 @@ def tile_attend_plq_assign_topk_kernel(tc, qT, k_words, k_scales, kn, qn, offs, 
                 nc.vector.tensor_copy(dst, src)
             else:
                 nc.scalar.copy(dst, src)
-        for k in (1, 0, 2):
-            cols = spans[k]
-            nc.vector.quantize_mx(out=y_code[:, cols].bitcast(FP8X4), scales=y_scale[:, cols], in_=y_bf[k][:].rearrange("p i t -> p (i t)"))
+        for k, cols in ((1, spans[1]), (0, slice(0, HALF)), (0, slice(HALF, TAIL)), (2, spans[2])):
+            first = spans[k].start
+            nc.vector.quantize_mx(
+                out=y_code[:, cols].bitcast(FP8X4),
+                scales=y_scale[:, cols],
+                in_=y_bf[k][:, cols.start - first : cols.stop - first, :].rearrange("p i t -> p (i t)"),
+            )
         for cols in halves:
             nc.sync.dma_start(out=out_words[:, cols], in_=y_code[:, cols].bitcast(I32))
         for r in range(4):

@@ -19,7 +19,7 @@ ACT = mybir.ActivationFunctionType
 P = 128
 PACK = 4
 HALF = N // 2
-Q_SPLIT = 64
+Q_SPLIT = 56
 LOWEST = -3.0e38
 ROWS = 16
 TAIL = 320
@@ -37,7 +37,7 @@ def tile_attend_plq_assign_topk_kernel(tc, qT, k_words, k_scales, kn, qn, offs, 
         one = sb.tile([P, 1], F32, name="one")
         nc.vector.memset(one[:], 1.0)
         scale_pool = sb.tile([P, T], U8, name="scale_pool")
-        nc.sync.dma_start(out=scale_pool[P - ROWS : P, :].bitcast(I32), in_=k_scales[0].bitcast(I32))
+        nc.scalar.dma_start(out=scale_pool[P - ROWS : P, :].bitcast(I32), in_=k_scales[0].bitcast(I32))
         nc.gpsimd.memset(scale_pool[0 : P - ROWS, :].bitcast(I32), 0)
         kn_pool = sb.tile([P, T], F32, name="kn_pool")
         nc.sync.dma_start(out=kn_pool[P - 1 : P, :], in_=kn[0:1, :])
@@ -49,7 +49,7 @@ def tile_attend_plq_assign_topk_kernel(tc, qT, k_words, k_scales, kn, qn, offs, 
         nc.sync.dma_start(out=word_pool[:], in_=k_words[0].rearrange("p t r -> p (t r)").bitcast(I32))
 
         qn_cols = sb.tile([P, PACK], F32, name="qn_cols")
-        nc.sync.dma_start(out=qn_cols[:], in_=qn[0].rearrange("(p t) o -> p (t o)", t=PACK))
+        nc.scalar.dma_start(out=qn_cols[:], in_=qn[0].rearrange("(p t) o -> p (t o)", t=PACK))
 
         ident = sb.tile([P, P], F32, name="ident")
         make_identity(nc, ident[:])
@@ -108,7 +108,8 @@ def tile_attend_plq_assign_topk_kernel(tc, qT, k_words, k_scales, kn, qn, offs, 
 
         y = sb.tile([P, PACK, N], F32, name="y")
         out_rows = out_0.rearrange("(p t) i -> p t i", t=PACK)
-        dist = [sb.tile([P, N], F32, name="dist%d" % t) for t in range(PACK)]
+        dist_all = sb.tile([P, PACK * N], F32, name="dist_all")
+        dist = [dist_all[:, t * N : (t + 1) * N] for t in range(PACK)]
         root = [sb.tile([P, N], F32, name="root%d" % t) for t in range(PACK)]
         wt = [sb.tile([P, N], F32, name="wt%d" % t) for t in range(PACK)]
         total = [sb.tile([P, 1], F32, name="total%d" % t) for t in range(PACK)]
@@ -118,10 +119,8 @@ def tile_attend_plq_assign_topk_kernel(tc, qT, k_words, k_scales, kn, qn, offs, 
             t, cols = pieces[b]
             nc.vector.scalar_tensor_tensor(dist[t][:, cols], banks[b][:], qn_half[:, t : t + 1], kn_all[:, cols], ALU.subtract, ALU.subtract)
 
-        def clamp(b):
-            t, cols = pieces[b]
-            engine = nc.gpsimd if 2 <= b <= 4 else nc.vector
-            engine.tensor_scalar(dist[t][:, cols], dist[t][:, cols], 0.0, LOWEST, ALU.min, ALU.max)
+        def clamp(engine, first, last):
+            engine.tensor_scalar(dist_all[:, first:last], dist_all[:, first:last], 0.0, LOWEST, ALU.min, ALU.max)
 
         def roots(t, cols):
             nc.scalar.activation(root[t][:, cols], dist[t][:, cols], ACT.Abs_reciprocal_sqrt, bias=one[:], scale=-2.0)
@@ -133,19 +132,26 @@ def tile_attend_plq_assign_topk_kernel(tc, qT, k_words, k_scales, kn, qn, offs, 
             nc.vector.scalar_tensor_tensor(wt[t][:], root[t][:], 1.0, root[t][:], ALU.mult, ALU.mult, accum_out=total[t][:])
 
         def back(t):
-            nc.vector.reciprocal(inv[t][:], total[t][:])
             if t < PACK - 1:
+                nc.vector.reciprocal(inv[t][:], total[t][:])
                 nc.vector.tensor_scalar(y[:, t, :], wt[t][:], inv[t][:], None, ALU.mult)
             else:
-                nc.scalar.activation(y[:, t, TAIL:N], wt[t][:, TAIL:N], ACT.Copy, scale=inv[t][:])
-                nc.vector.tensor_scalar(y[:, t, 0:TAIL], wt[t][:, 0:TAIL], inv[t][:], None, ALU.mult)
+                nc.scalar.activation(inv[t][:], total[t][:], ACT.Abs_reciprocal_sqrt)
+                nc.scalar.activation(y[:, t, TAIL:N], root[t][:, TAIL:N], ACT.Square, scale=inv[t][:])
+                nc.vector.tensor_scalar(y[:, t, 0:TAIL], wt[t][:, 0:TAIL], inv[t][:], inv[t][:], ALU.mult, ALU.mult)
             nc.sync.dma_start(out=out_rows[:, t, :], in_=y[:, t, :])
 
-        for b in range(0, len(pieces), 2):
-            cross(b)
-            cross(b + 1)
-            clamp(b)
-            clamp(b + 1)
+        cross(0)
+        cross(1)
+        clamp(nc.vector, 0, HALF)
+        clamp(nc.gpsimd, N, N + HALF)
+        cross(2)
+        cross(3)
+        clamp(nc.gpsimd, HALF, N)
+        clamp(nc.gpsimd, N + HALF, 2 * N)
+        cross(4)
+        cross(5)
+        clamp(nc.vector, 2 * N, PACK * N)
         for t, cols in pieces[0:4]:
             roots(t, cols)
         squares(0)

@@ -19,7 +19,7 @@ ACT = mybir.ActivationFunctionType
 P = 128
 PACK = 4
 HALF = N // 2
-Q_SPLIT = 56
+Q_SPLIT = 64
 LOWEST = -3.0e38
 ROWS = 16
 TAIL = 320
@@ -37,7 +37,7 @@ def tile_attend_plq_assign_topk_kernel(tc, qT, k_words, k_scales, kn, qn, offs, 
         one = sb.tile([P, 1], F32, name="one")
         nc.vector.memset(one[:], 1.0)
         scale_pool = sb.tile([P, T], U8, name="scale_pool")
-        nc.scalar.dma_start(out=scale_pool[P - ROWS : P, :].bitcast(I32), in_=k_scales[0].bitcast(I32))
+        nc.sync.dma_start(out=scale_pool[P - ROWS : P, :].bitcast(I32), in_=k_scales[0].bitcast(I32))
         nc.gpsimd.memset(scale_pool[0 : P - ROWS, :].bitcast(I32), 0)
         kn_pool = sb.tile([P, T], F32, name="kn_pool")
         nc.sync.dma_start(out=kn_pool[P - 1 : P, :], in_=kn[0:1, :])
@@ -49,7 +49,7 @@ def tile_attend_plq_assign_topk_kernel(tc, qT, k_words, k_scales, kn, qn, offs, 
         nc.sync.dma_start(out=word_pool[:], in_=k_words[0].rearrange("p t r -> p (t r)").bitcast(I32))
 
         qn_cols = sb.tile([P, PACK], F32, name="qn_cols")
-        nc.scalar.dma_start(out=qn_cols[:], in_=qn[0].rearrange("(p t) o -> p (t o)", t=PACK))
+        nc.sync.dma_start(out=qn_cols[:], in_=qn[0].rearrange("(p t) o -> p (t o)", t=PACK))
 
         ident = sb.tile([P, P], F32, name="ident")
         make_identity(nc, ident[:])

@@ -62,7 +62,7 @@ def tile_attend_plq_assign_topk_kernel(tc, qT, k_words, k_scales, kn, qn, offs, 
         nc.gpsimd.memset(k_scale[:].bitcast(I32), 0)
         for quad in range(4):
             first = P - ROWS + 4 * quad
-            nc.scalar.dma_start(out=k_scale[32 * quad : 32 * quad + 4, :].bitcast(I32), in_=picked[first : first + 4, :].bitcast(I32))
+            nc.sync.dma_start(out=k_scale[32 * quad : 32 * quad + 4, :].bitcast(I32), in_=picked[first : first + 4, :].bitcast(I32))
 
         kn_row = sb.tile([P, N], F32, name="kn_row")
         nc.vector.tensor_copy(kn_row[:], kn_pool[:].indirect(offsets[:]))
@@ -186,5 +186,4 @@ def tile_attend_plq_assign_topk_kernel(tc, qT, k_words, k_scales, kn, qn, offs, 
         for cols in halves:
             nc.sync.dma_start(out=out_words[:, cols], in_=y_code[:, cols].bitcast(I32))
         for r in range(4):
-            queue = nc.scalar if r % 2 == 0 else nc.sync
-            queue.dma_start(out=out_2[0, r:16:4, :].bitcast(I32), in_=y_scale[r:P:32, :].bitcast(I32))
+            nc.sync.dma_start(out=out_2[0, r:16:4, :].bitcast(I32), in_=y_scale[r:P:32, :].bitcast(I32))

@@ -48,8 +48,6 @@ def tile_attend_plq_assign_topk_kernel(tc, qT, k_words, k_scales, kn, qn, offs, 
         word_pool = sb.tile([P, T], I32, name="word_pool")
         nc.sync.dma_start(out=word_pool[:], in_=k_words[0].rearrange("p t r -> p (t r)").bitcast(I32))
 
-        qn_cols = sb.tile([P, PACK], F32, name="qn_cols")
-        nc.sync.dma_start(out=qn_cols[:], in_=qn[0].rearrange("(p t) o -> p (t o)", t=PACK))
 
         ident = sb.tile([P, P], F32, name="ident")
         make_identity(nc, ident[:])
@@ -63,6 +61,9 @@ def tile_attend_plq_assign_topk_kernel(tc, qT, k_words, k_scales, kn, qn, offs, 
         for quad in range(4):
             first = P - ROWS + 4 * quad
             nc.sync.dma_start(out=k_scale[32 * quad : 32 * quad + 4, :].bitcast(I32), in_=picked[first : first + 4, :].bitcast(I32))
+
+        qn_cols = sb.tile([P, PACK], F32, name="qn_cols", tag="scale_pool")
+        nc.sync.dma_start(out=qn_cols[:], in_=qn[0].rearrange("(p t) o -> p (t o)", t=PACK))
 
         kn_row = sb.tile([P, N], F32, name="kn_row")
         nc.vector.tensor_copy(kn_row[:], kn_pool[:].indirect(offsets[:]))
@@ -151,7 +152,8 @@ def tile_attend_plq_assign_topk_kernel(tc, qT, k_words, k_scales, kn, qn, offs, 
         clamp(nc.gpsimd, N + HALF, 2 * N)
         cross(4)
         cross(5)
-        clamp(nc.vector, 2 * N, PACK * N)
+        clamp(nc.vector, 2 * N, 3 * N)
+        clamp(nc.vector, 3 * N, PACK * N)
         for t, cols in pieces[0:4]:
             roots(t, cols)
         squares(0)

@@ -19,7 +19,7 @@ ACT = mybir.ActivationFunctionType
 P = 128
 PACK = 4
 HALF = N // 2
-Q_SPLIT = 64
+Q_SPLIT = 52
 LOWEST = -3.0e38
 ROWS = 16
 TAIL = 320

@@ -23,6 +23,7 @@ Q_SPLIT = 52
 LOWEST = -3.0e38
 ROWS = 16
 TAIL = 320
+LAST = 96
 
 
 def tile_attend_plq_assign_topk_kernel(tc, qT, k_words, k_scales, kn, qn, offs, out_0, out_1, out_2):
@@ -66,7 +67,7 @@ def tile_attend_plq_assign_topk_kernel(tc, qT, k_words, k_scales, kn, qn, offs, 
         nc.sync.dma_start(out=qn_cols[:], in_=qn[0].rearrange("(p t) o -> p (t o)", t=PACK))
 
         kn_row = sb.tile([P, N], F32, name="kn_row")
-        nc.vector.tensor_copy(kn_row[:], kn_pool[:].indirect(offsets[:]))
+        nc.scalar.activation(kn_row[:], kn_pool[:].indirect(offsets[:]), ACT.Copy)
         kn_turned = ps.tile([P, PACK, P], F32, name="kn_turned")
         for j in range(PACK):
             nc.tensor.transpose(kn_turned[:, j, :], kn_row[:, j * P : (j + 1) * P], ident[:])
@@ -138,8 +139,8 @@ def tile_attend_plq_assign_topk_kernel(tc, qT, k_words, k_scales, kn, qn, offs, 
                 nc.vector.tensor_scalar(y[:, t, :], wt[t][:], inv[t][:], None, ALU.mult)
             else:
                 nc.scalar.activation(inv[t][:], total[t][:], ACT.Abs_reciprocal_sqrt)
-                nc.scalar.activation(y[:, t, TAIL:N], root[t][:, TAIL:N], ACT.Square, scale=inv[t][:])
-                nc.vector.tensor_scalar(y[:, t, 0:TAIL], wt[t][:, 0:TAIL], inv[t][:], inv[t][:], ALU.mult, ALU.mult)
+                nc.scalar.activation(y[:, t, 0 : N - TAIL], root[t][:, 0 : N - TAIL], ACT.Square, scale=inv[t][:])
+                nc.vector.tensor_scalar(y[:, t, N - TAIL : N], wt[t][:, N - TAIL : N], inv[t][:], inv[t][:], ALU.mult, ALU.mult)
             nc.sync.dma_start(out=out_rows[:, t, :], in_=y[:, t, :])
 
         cross(0)
@@ -169,23 +170,12 @@ def tile_attend_plq_assign_topk_kernel(tc, qT, k_words, k_scales, kn, qn, offs, 
         y_code = sb.tile([P, N], U32, name="y_code", align_bytes=64)
         y_scale = sb.tile([P, N], U8, name="y_scale", align_bytes=64)
         out_words = out_1[0].rearrange("p i u -> p (i u)").bitcast(I32)
-        spans = [slice(0, TAIL), slice(TAIL, TAIL + P), slice(TAIL + P, N)]
-        y_bf = [sb.tile([P, c.stop - c.start, PACK], BF16, name="y_bf%d" % c.start, align_bytes=64) for c in spans]
-        for k, cols in enumerate(spans):
-            dst = y_bf[k][:].rearrange("p (c i) t -> p c t i", i=4)
-            src = y[:, :, cols].rearrange("p t (c i) -> p c t i", i=4)
-            if k == 0:
-                nc.vector.tensor_copy(dst, src)
-            else:
-                nc.scalar.copy(dst, src)
-        for k, cols in ((1, spans[1]), (0, slice(0, HALF)), (0, slice(HALF, TAIL)), (2, spans[2])):
-            first = spans[k].start
-            nc.vector.quantize_mx(
-                out=y_code[:, cols].bitcast(FP8X4),
-                scales=y_scale[:, cols],
-                in_=y_bf[k][:, cols.start - first : cols.stop - first, :].rearrange("p i t -> p (i t)"),
-            )
-        for cols in halves:
+        y_bf = sb.tile([P, N, PACK], BF16, name="y_bf", align_bytes=64)
+        for copy, cols in ((nc.scalar.copy, slice(0, P)), (nc.vector.tensor_copy, slice(P, N - LAST)), (nc.scalar.copy, slice(N - LAST, N))):
+            copy(y_bf[:, cols, :].rearrange("p (c i) t -> p c t i", i=4), y[:, :, cols].rearrange("p t (c i) -> p c t i", i=4))
+        for cols in (slice(0, P), slice(P, 3 * P), slice(3 * P, N)):
+            nc.vector.quantize_mx(out=y_code[:, cols].bitcast(FP8X4), scales=y_scale[:, cols], in_=y_bf[:, cols, :].rearrange("p i t -> p (i t)"))
+        for cols in (slice(0, 3 * P), slice(3 * P, N)):
             nc.sync.dma_start(out=out_words[:, cols], in_=y_code[:, cols].bitcast(I32))
         for r in range(4):
             nc.sync.dma_start(out=out_2[0, r:16:4, :].bitcast(I32), in_=y_scale[r:P:32, :].bitcast(I32))

@@ -149,23 +149,32 @@ def tile_attend_plq_assign_topk_kernel(tc, qT, k_words, k_scales, kn, qn, offs, 
         clamp(nc.gpsimd, N, N + HALF)
         cross(2)
         cross(3)
-        clamp(nc.gpsimd, HALF, N)
+        clamp(nc.vector, HALF, N)
         clamp(nc.gpsimd, N + HALF, 2 * N)
         cross(4)
+        clamp(nc.gpsimd, 2 * N, 2 * N + HALF)
         cross(5)
-        clamp(nc.vector, 2 * N, 3 * N)
+        clamp(nc.vector, 2 * N + HALF, 3 * N)
         clamp(nc.vector, 3 * N, PACK * N)
-        for t, cols in pieces[0:4]:
-            roots(t, cols)
+        for b in (0, 2, 1):
+            roots(*pieces[b])
         squares(0)
+        roots(*pieces[3])
+        nc.vector.reciprocal(inv[0][:], total[0][:])
+        rest = sb.tile([P, 1], F32, name="rest")
+        nc.scalar.activation(wt[1][:, 0:P], root[1][:, 0:P], ACT.Square, accum_out=total[1][:])
+        nc.vector.scalar_tensor_tensor(wt[1][:, P:N], root[1][:, P:N], 1.0, root[1][:, P:N], ALU.mult, ALU.mult, accum_out=rest[:])
         roots(2, slice(0, N))
+        nc.scalar.activation(inv[1][:], total[1][:], ACT.Abs_reciprocal_sqrt, bias=rest[:])
         roots(3, slice(0, N))
-        squares_on_vector(1)
-        back(0)
+        nc.vector.tensor_scalar(y[:, 0, :], wt[0][:], inv[0][:], None, ALU.mult)
+        nc.sync.dma_start(out=out_rows[:, 0, :], in_=y[:, 0, :])
+        nc.vector.tensor_scalar(y[:, 1, :], wt[1][:], inv[1][:], inv[1][:], ALU.mult, ALU.mult)
+        nc.sync.dma_start(out=out_rows[:, 1, :], in_=y[:, 1, :])
         squares_on_vector(2)
         squares(3)
-        for t in range(1, PACK):
-            back(t)
+        back(2)
+        back(3)
 
         y_code = sb.tile([P, N], U32, name="y_code", align_bytes=64)
         y_scale = sb.tile([P, N], U8, name="y_scale", align_bytes=64)

@@ -22,8 +22,10 @@ HALF = N // 2
 Q_SPLIT = 52
 LOWEST = -3.0e38
 ROWS = 16
-TAIL = 320
-LAST = 96
+TAIL = 192
+LAST = 128
+SHARE = 128
+SHRINK = 2.0 ** -20
 
 
 def tile_attend_plq_assign_topk_kernel(tc, qT, k_words, k_scales, kn, qn, offs, out_0, out_1, out_2):
@@ -79,7 +81,7 @@ def tile_attend_plq_assign_topk_kernel(tc, qT, k_words, k_scales, kn, qn, offs, 
         kn_all = sb.tile([P, N], F32, name="kn_all")
         nc.scalar.activation(kn_all[:], kn_spread[:], ACT.Copy, scale=0.5)
         qn_half = sb.tile([P, PACK], F32, name="qn_half")
-        nc.scalar.activation(qn_half[:], qn_cols[:], ACT.Copy, scale=0.5)
+        nc.scalar.activation(qn_half[:], qn_cols[:], ACT.Copy, scale=0.5, bias=0.5)
 
         q_bf = sb.tile([P, PACK, P, PACK], BF16, name="q_bf", align_bytes=64)
         q_dst = q_bf[:].rearrange("p t m j -> p m j t")
@@ -112,7 +114,7 @@ def tile_attend_plq_assign_topk_kernel(tc, qT, k_words, k_scales, kn, qn, offs, 
         out_rows = out_0.rearrange("(p t) i -> p t i", t=PACK)
         dist_all = sb.tile([P, PACK * N], F32, name="dist_all")
         dist = [dist_all[:, t * N : (t + 1) * N] for t in range(PACK)]
-        root = [sb.tile([P, N], F32, name="root%d" % t) for t in range(PACK)]
+        sq_all = sb.tile([P, PACK * N], F32, name="sq_all")
         wt = [sb.tile([P, N], F32, name="wt%d" % t) for t in range(PACK)]
         total = [sb.tile([P, 1], F32, name="total%d" % t) for t in range(PACK)]
         inv = [sb.tile([P, 1], F32, name="inv%d" % t) for t in range(PACK)]
@@ -122,25 +124,19 @@ def tile_attend_plq_assign_topk_kernel(tc, qT, k_words, k_scales, kn, qn, offs, 
             nc.vector.scalar_tensor_tensor(dist[t][:, cols], banks[b][:], qn_half[:, t : t + 1], kn_all[:, cols], ALU.subtract, ALU.subtract)
 
         def clamp(engine, first, last):
-            engine.tensor_scalar(dist_all[:, first:last], dist_all[:, first:last], 0.0, LOWEST, ALU.min, ALU.max)
+            engine.tensor_scalar(dist_all[:, first:last], dist_all[:, first:last], -0.5, LOWEST, ALU.min, ALU.max)
 
-        def roots(t, cols):
-            nc.scalar.activation(root[t][:, cols], dist[t][:, cols], ACT.Abs_reciprocal_sqrt, bias=one[:], scale=-2.0)
+        def square_on_scalar(first, last):
+            nc.scalar.activation(sq_all[:, first:last], dist_all[:, first:last], ACT.Square, scale=SHRINK)
 
-        def squares(t):
-            nc.scalar.activation(wt[t][:], root[t][:], ACT.Square, accum_out=total[t][:])
+        def square_on_vector(first, last):
+            nc.vector.scalar_tensor_tensor(sq_all[:, first:last], dist_all[:, first:last], SHRINK * SHRINK, dist_all[:, first:last], ALU.mult, ALU.mult)
 
-        def squares_on_vector(t):
-            nc.vector.scalar_tensor_tensor(wt[t][:], root[t][:], 1.0, root[t][:], ALU.mult, ALU.mult, accum_out=total[t][:])
+        def weights(t):
+            nc.scalar.activation(wt[t][:], sq_all[:, t * N : (t + 1) * N], ACT.Abs_reciprocal_sqrt, accum_out=total[t][:])
 
-        def back(t):
-            if t < PACK - 1:
-                nc.vector.reciprocal(inv[t][:], total[t][:])
-                nc.vector.tensor_scalar(y[:, t, :], wt[t][:], inv[t][:], None, ALU.mult)
-            else:
-                nc.scalar.activation(inv[t][:], total[t][:], ACT.Abs_reciprocal_sqrt)
-                nc.scalar.activation(y[:, t, 0 : N - TAIL], root[t][:, 0 : N - TAIL], ACT.Square, scale=inv[t][:])
-                nc.vector.tensor_scalar(y[:, t, N - TAIL : N], wt[t][:, N - TAIL : N], inv[t][:], inv[t][:], ALU.mult, ALU.mult)
+        def normed(t):
+            nc.vector.tensor_scalar(y[:, t, :], wt[t][:], inv[t][:], None, ALU.mult)
             nc.sync.dma_start(out=out_rows[:, t, :], in_=y[:, t, :])
 
         cross(0)
@@ -156,25 +152,28 @@ def tile_attend_plq_assign_topk_kernel(tc, qT, k_words, k_scales, kn, qn, offs, 
         cross(5)
         clamp(nc.vector, 2 * N + HALF, 3 * N)
         clamp(nc.vector, 3 * N, PACK * N)
-        for b in (0, 2, 1):
-            roots(*pieces[b])
-        squares(0)
-        roots(*pieces[3])
+        square_on_scalar(0, HALF)
+        square_on_scalar(N, N + HALF)
+        square_on_scalar(HALF, N)
+        square_on_scalar(N + HALF, 2 * N)
+        weights(0)
+        square_on_scalar(2 * N, 2 * N + SHARE)
+        weights(1)
+        square_on_vector(2 * N + SHARE, 3 * N)
         nc.vector.reciprocal(inv[0][:], total[0][:])
-        rest = sb.tile([P, 1], F32, name="rest")
-        nc.scalar.activation(wt[1][:, 0:P], root[1][:, 0:P], ACT.Square, accum_out=total[1][:])
-        nc.vector.scalar_tensor_tensor(wt[1][:, P:N], root[1][:, P:N], 1.0, root[1][:, P:N], ALU.mult, ALU.mult, accum_out=rest[:])
-        roots(2, slice(0, N))
-        nc.scalar.activation(inv[1][:], total[1][:], ACT.Abs_reciprocal_sqrt, bias=rest[:])
-        roots(3, slice(0, N))
-        nc.vector.tensor_scalar(y[:, 0, :], wt[0][:], inv[0][:], None, ALU.mult)
-        nc.sync.dma_start(out=out_rows[:, 0, :], in_=y[:, 0, :])
-        nc.vector.tensor_scalar(y[:, 1, :], wt[1][:], inv[1][:], inv[1][:], ALU.mult, ALU.mult)
-        nc.sync.dma_start(out=out_rows[:, 1, :], in_=y[:, 1, :])
-        squares_on_vector(2)
-        squares(3)
-        back(2)
-        back(3)
+        square_on_vector(3 * N, PACK * N)
+        weights(2)
+        weights(3)
+        nc.vector.reciprocal(inv[1][:], total[1][:])
+        normed(0)
+        nc.vector.reciprocal(inv[2][:], total[2][:])
+        normed(1)
+        last = PACK - 1
+        nc.vector.reciprocal(inv[last][:], total[last][:])
+        normed(2)
+        nc.scalar.activation(y[:, last, 0 : N - TAIL], wt[last][:, 0 : N - TAIL], ACT.Copy, scale=inv[last][:])
+        nc.vector.tensor_scalar(y[:, last, N - TAIL : N], wt[last][:, N - TAIL : N], inv[last][:], None, ALU.mult)
+        nc.sync.dma_start(out=out_rows[:, last, :], in_=y[:, last, :])
 
         y_code = sb.tile([P, N], U32, name="y_code", align_bytes=64)
         y_scale = sb.tile([P, N], U8, name="y_scale", align_bytes=64)

@@ -22,9 +22,9 @@ HALF = N // 2
 Q_SPLIT = 52
 LOWEST = -3.0e38
 ROWS = 16
-TAIL = 192
+TAIL = 224
 LAST = 128
-SHARE = 128
+SHARE = 192
 SHRINK = 2.0 ** -20
 
 
@@ -94,14 +94,16 @@ def tile_attend_plq_assign_topk_kernel(tc, qT, k_words, k_scales, kn, qn, offs, 
 
         k_code = sb.tile([P, N], U32, name="k_code", align_bytes=64)
         halves = [slice(0, HALF), slice(HALF, N)]
-        for h in range(2):
-            nc.vector.tensor_copy(k_code[:, halves[h]], word_pool[:].bitcast(U32).indirect(offsets[:, 16 * h : 16 * (h + 1)]))
+        for first, last in ((0, P), (P, HALF), (HALF, N)):
+            nc.vector.tensor_copy(k_code[:, first:last], word_pool[:].bitcast(U32).indirect(offsets[:, first // 16 : last // 16]))
 
         pieces = [(t, cols) for cols in halves for t in range(2)] + [(t, slice(0, N)) for t in range(2, PACK)]
         banks = [ps.tile([P, cols.stop - cols.start], F32, name="bank%d" % b) for b, (t, cols) in enumerate(pieces)]
-        for bank, (t, cols) in zip(banks, pieces):
+        products = [(banks[t][:, cols], t, cols) for cols in (slice(0, P), slice(P, HALF)) for t in range(2)]
+        products += [(bank[:], t, cols) for bank, (t, cols) in zip(banks[2:], pieces[2:])]
+        for out, t, cols in products:
             nc.tensor.matmul_mx(
-                out=bank[:],
+                out=out,
                 lhsT=q_code[:, t * P : (t + 1) * P].bitcast(FP8X4),
                 lhsT_scale=q_scale[:, t * P : (t + 1) * P],
                 rhs=k_code[:, cols].bitcast(FP8X4),
@@ -171,7 +173,8 @@ def tile_attend_plq_assign_topk_kernel(tc, qT, k_words, k_scales, kn, qn, offs, 
         last = PACK - 1
         nc.vector.reciprocal(inv[last][:], total[last][:])
         normed(2)
-        nc.scalar.activation(y[:, last, 0 : N - TAIL], wt[last][:, 0 : N - TAIL], ACT.Copy, scale=inv[last][:])
+        for cols in (slice(0, P), slice(P, N - TAIL)):
+            nc.scalar.activation(y[:, last, cols], wt[last][:, cols], ACT.Copy, scale=inv[last][:])
         nc.vector.tensor_scalar(y[:, last, N - TAIL : N], wt[last][:, N - TAIL : N], inv[last][:], None, ALU.mult)
         nc.sync.dma_start(out=out_rows[:, last, :], in_=y[:, last, :])
 

@@ -22,10 +22,9 @@ HALF = N // 2
 Q_SPLIT = 52
 LOWEST = -3.0e38
 ROWS = 16
-TAIL = 224
 LAST = 128
 SHARE = 192
-SHRINK = 2.0 ** -20
+SHRINK = 2.0 ** -16
 
 
 def tile_attend_plq_assign_topk_kernel(tc, qT, k_words, k_scales, kn, qn, offs, out_0, out_1, out_2):
@@ -168,14 +167,14 @@ def tile_attend_plq_assign_topk_kernel(tc, qT, k_words, k_scales, kn, qn, offs, 
         weights(3)
         nc.vector.reciprocal(inv[1][:], total[1][:])
         normed(0)
-        nc.vector.reciprocal(inv[2][:], total[2][:])
         normed(1)
+        nc.vector.reciprocal(inv[2][:], total[2][:])
         last = PACK - 1
         nc.vector.reciprocal(inv[last][:], total[last][:])
         normed(2)
-        for cols in (slice(0, P), slice(P, N - TAIL)):
+        for cols in (slice(0, P), slice(N - LAST, N)):
             nc.scalar.activation(y[:, last, cols], wt[last][:, cols], ACT.Copy, scale=inv[last][:])
-        nc.vector.tensor_scalar(y[:, last, N - TAIL : N], wt[last][:, N - TAIL : N], inv[last][:], None, ALU.mult)
+        nc.vector.tensor_scalar(y[:, last, P : N - LAST], wt[last][:, P : N - LAST], inv[last][:], None, ALU.mult)
         nc.sync.dma_start(out=out_rows[:, last, :], in_=y[:, last, :])
 
         y_code = sb.tile([P, N], U32, name="y_code", align_bytes=64)

@@ -22,7 +22,7 @@ HALF = N // 2
 Q_SPLIT = 52
 LOWEST = -3.0e38
 ROWS = 16
-LAST = 128
+LAST = 96
 SHARE = 192
 SHRINK = 2.0 ** -16
 
@@ -149,9 +149,9 @@ def tile_attend_plq_assign_topk_kernel(tc, qT, k_words, k_scales, kn, qn, offs, 
         clamp(nc.vector, HALF, N)
         clamp(nc.gpsimd, N + HALF, 2 * N)
         cross(4)
-        clamp(nc.gpsimd, 2 * N, 2 * N + HALF)
+        clamp(nc.gpsimd, 2 * N, 2 * N + SHARE)
         cross(5)
-        clamp(nc.vector, 2 * N + HALF, 3 * N)
+        clamp(nc.vector, 2 * N + SHARE, 3 * N)
         clamp(nc.vector, 3 * N, PACK * N)
         square_on_scalar(0, HALF)
         square_on_scalar(N, N + HALF)

@@ -20,10 +20,10 @@ P = 128
 PACK = 4
 HALF = N // 2
 Q_SPLIT = 52
-LOWEST = -3.0e38
+LOWEST = -(2.0 ** 79)
 ROWS = 16
 LAST = 96
-SHARE = 192
+SHARE = 128
 SHRINK = 2.0 ** -16
 
 

@@ -20,11 +20,11 @@ P = 128
 PACK = 4
 HALF = N // 2
 Q_SPLIT = 52
-LOWEST = -(2.0 ** 79)
+LOWEST = -(2.0 ** 80)
 ROWS = 16
 LAST = 96
 SHARE = 128
-SHRINK = 2.0 ** -16
+SHRINK = 2.0 ** -17
 
 
 def tile_attend_plq_assign_topk_kernel(tc, qT, k_words, k_scales, kn, qn, offs, out_0, out_1, out_2):
@@ -78,28 +78,33 @@ def tile_attend_plq_assign_topk_kernel(tc, qT, k_words, k_scales, kn, qn, offs, 
         for j in range(PACK):
             nc.tensor.transpose(kn_spread[:, j * P : (j + 1) * P], kn_cols[:, j : j + 1].to_broadcast([P, P]), ident[:])
         kn_all = sb.tile([P, N], F32, name="kn_all")
-        nc.scalar.activation(kn_all[:], kn_spread[:], ACT.Copy, scale=0.5)
-        qn_half = sb.tile([P, PACK], F32, name="qn_half")
-        nc.scalar.activation(qn_half[:], qn_cols[:], ACT.Copy, scale=0.5, bias=0.5)
+        nc.scalar.activation(kn_all[:], kn_spread[:], ACT.Copy, bias=1.0)
 
         q_bf = sb.tile([P, PACK, P, PACK], BF16, name="q_bf", align_bytes=64)
         q_dst = q_bf[:].rearrange("p t m j -> p m j t")
         q_src = q_raw[:].rearrange("p j (m t) -> p m j t", t=PACK)
-        nc.scalar.copy(q_dst[:, 0:Q_SPLIT], q_src[:, 0:Q_SPLIT])
-        nc.vector.tensor_copy(q_dst[:, Q_SPLIT:P], q_src[:, Q_SPLIT:P])
+        nc.scalar.activation(q_dst[:, 0:Q_SPLIT], q_src[:, 0:Q_SPLIT], ACT.Copy, scale=2.0)
+        nc.vector.tensor_scalar(q_dst[:, Q_SPLIT:P], q_src[:, Q_SPLIT:P], 2.0, None, ALU.mult)
         q_code = sb.tile([P, NQ], U32, name="q_code", align_bytes=64)
         q_scale = sb.tile([P, NQ], U8, name="q_scale", align_bytes=64)
         nc.vector.quantize_mx(out=q_code[:].bitcast(FP8X4), scales=q_scale[:], in_=q_bf[:].rearrange("p t m j -> p (t m j)"))
 
         k_code = sb.tile([P, N], U32, name="k_code", align_bytes=64)
         halves = [slice(0, HALF), slice(HALF, N)]
-        for first, last in ((0, P), (P, HALF), (HALF, N)):
+        quarters = [slice(j * P, (j + 1) * P) for j in range(PACK)]
+        for first, last in [(cols.start, cols.stop) for cols in quarters]:
             nc.vector.tensor_copy(k_code[:, first:last], word_pool[:].bitcast(U32).indirect(offsets[:, first // 16 : last // 16]))
 
-        pieces = [(t, cols) for cols in halves for t in range(2)] + [(t, slice(0, N)) for t in range(2, PACK)]
-        banks = [ps.tile([P, cols.stop - cols.start], F32, name="bank%d" % b) for b, (t, cols) in enumerate(pieces)]
-        products = [(banks[t][:, cols], t, cols) for cols in (slice(0, P), slice(P, HALF)) for t in range(2)]
-        products += [(bank[:], t, cols) for bank, (t, cols) in zip(banks[2:], pieces[2:])]
+        pieces = [(0, quarters[0]), (0, quarters[1]), (1, halves[0]), (0, halves[1]), (1, halves[1]), (2, slice(0, N)), (3, slice(0, N))]
+        tags = ["bank%d" % b for b in range(len(pieces) - 1)] + ["kn_turned"]
+        banks = [ps.tile([P, cols.stop - cols.start], F32, name="bank%d" % b, tag=tags[b]) for b, (t, cols) in enumerate(pieces)]
+        products = []
+        for cols in quarters:
+            for t in range(2):
+                b = [b for b, (u, span) in enumerate(pieces) if u == t and span.start <= cols.start < span.stop][0]
+                first = cols.start - pieces[b][1].start
+                products.append((banks[b][:, first : first + P], t, cols))
+        products += [(banks[b][:], t, cols) for b, (t, cols) in enumerate(pieces) if t >= 2]
         for out, t, cols in products:
             nc.tensor.matmul_mx(
                 out=out,
@@ -122,10 +127,10 @@ def tile_attend_plq_assign_topk_kernel(tc, qT, k_words, k_scales, kn, qn, offs, 
 
         def cross(b):
             t, cols = pieces[b]
-            nc.vector.scalar_tensor_tensor(dist[t][:, cols], banks[b][:], qn_half[:, t : t + 1], kn_all[:, cols], ALU.subtract, ALU.subtract)
+            nc.vector.scalar_tensor_tensor(dist[t][:, cols], banks[b][:], qn_cols[:, t : t + 1], kn_all[:, cols], ALU.subtract, ALU.subtract)
 
         def clamp(engine, first, last):
-            engine.tensor_scalar(dist_all[:, first:last], dist_all[:, first:last], -0.5, LOWEST, ALU.min, ALU.max)
+            engine.tensor_scalar(dist_all[:, first:last], dist_all[:, first:last], -1.0, LOWEST, ALU.min, ALU.max)
 
         def square_on_scalar(first, last):
             nc.scalar.activation(sq_all[:, first:last], dist_all[:, first:last], ACT.Square, scale=SHRINK)
@@ -142,15 +147,16 @@ def tile_attend_plq_assign_topk_kernel(tc, qT, k_words, k_scales, kn, qn, offs, 
 
         cross(0)
         cross(1)
+        cross(2)
         clamp(nc.vector, 0, HALF)
         clamp(nc.gpsimd, N, N + HALF)
-        cross(2)
         cross(3)
+        cross(4)
         clamp(nc.vector, HALF, N)
         clamp(nc.gpsimd, N + HALF, 2 * N)
-        cross(4)
-        clamp(nc.gpsimd, 2 * N, 2 * N + SHARE)
         cross(5)
+        clamp(nc.gpsimd, 2 * N, 2 * N + SHARE)
+        cross(6)
         clamp(nc.vector, 2 * N + SHARE, 3 * N)
         clamp(nc.vector, 3 * N, PACK * N)
         square_on_scalar(0, HALF)

@@ -95,16 +95,11 @@ def tile_attend_plq_assign_topk_kernel(tc, qT, k_words, k_scales, kn, qn, offs, 
         for first, last in [(cols.start, cols.stop) for cols in quarters]:
             nc.vector.tensor_copy(k_code[:, first:last], word_pool[:].bitcast(U32).indirect(offsets[:, first // 16 : last // 16]))
 
-        pieces = [(0, quarters[0]), (0, quarters[1]), (1, halves[0]), (0, halves[1]), (1, halves[1]), (2, slice(0, N)), (3, slice(0, N))]
-        tags = ["bank%d" % b for b in range(len(pieces) - 1)] + ["kn_turned"]
-        banks = [ps.tile([P, cols.stop - cols.start], F32, name="bank%d" % b, tag=tags[b]) for b, (t, cols) in enumerate(pieces)]
-        products = []
-        for cols in quarters:
-            for t in range(2):
-                b = [b for b, (u, span) in enumerate(pieces) if u == t and span.start <= cols.start < span.stop][0]
-                first = cols.start - pieces[b][1].start
-                products.append((banks[b][:, first : first + P], t, cols))
-        products += [(banks[b][:], t, cols) for b, (t, cols) in enumerate(pieces) if t >= 2]
+        pieces = [(t, cols) for cols in halves for t in range(2)] + [(t, slice(0, N)) for t in range(2, PACK)]
+        banks = [ps.tile([P, cols.stop - cols.start], F32, name="bank%d" % b) for b, (t, cols) in enumerate(pieces)]
+        products = [(banks[0][:, cols], 0, cols) for cols in quarters[0:2]] + [(banks[1][:], 1, halves[0])]
+        products += [(banks[2][:, cols.start - HALF : cols.stop - HALF], 0, cols) for cols in quarters[2:4]]
+        products += [(bank[:], t, cols) for bank, (t, cols) in zip(banks[3:], pieces[3:])]
         for out, t, cols in products:
             nc.tensor.matmul_mx(
                 out=out,
@@ -147,16 +142,15 @@ def tile_attend_plq_assign_topk_kernel(tc, qT, k_words, k_scales, kn, qn, offs, 
 
         cross(0)
         cross(1)
-        cross(2)
         clamp(nc.vector, 0, HALF)
         clamp(nc.gpsimd, N, N + HALF)
+        cross(2)
         cross(3)
-        cross(4)
         clamp(nc.vector, HALF, N)
         clamp(nc.gpsimd, N + HALF, 2 * N)
-        cross(5)
+        cross(4)
         clamp(nc.gpsimd, 2 * N, 2 * N + SHARE)
-        cross(6)
+        cross(5)
         clamp(nc.vector, 2 * N + SHARE, 3 * N)
         clamp(nc.vector, 3 * N, PACK * N)
         square_on_scalar(0, HALF)

@@ -23,7 +23,8 @@ Q_SPLIT = 52
 LOWEST = -(2.0 ** 80)
 ROWS = 16
 LAST = 96
-SHARE = 128
+SHARE = 192
+HELP = 128
 SHRINK = 2.0 ** -17
 
 
@@ -91,15 +92,14 @@ def tile_attend_plq_assign_topk_kernel(tc, qT, k_words, k_scales, kn, qn, offs, 
 
         k_code = sb.tile([P, N], U32, name="k_code", align_bytes=64)
         halves = [slice(0, HALF), slice(HALF, N)]
-        quarters = [slice(j * P, (j + 1) * P) for j in range(PACK)]
-        for first, last in [(cols.start, cols.stop) for cols in quarters]:
+        for first, last in ((0, P), (P, HALF), (HALF, N)):
             nc.vector.tensor_copy(k_code[:, first:last], word_pool[:].bitcast(U32).indirect(offsets[:, first // 16 : last // 16]))
 
-        pieces = [(t, cols) for cols in halves for t in range(2)] + [(t, slice(0, N)) for t in range(2, PACK)]
-        banks = [ps.tile([P, cols.stop - cols.start], F32, name="bank%d" % b) for b, (t, cols) in enumerate(pieces)]
-        products = [(banks[0][:, cols], 0, cols) for cols in quarters[0:2]] + [(banks[1][:], 1, halves[0])]
-        products += [(banks[2][:, cols.start - HALF : cols.stop - HALF], 0, cols) for cols in quarters[2:4]]
-        products += [(bank[:], t, cols) for bank, (t, cols) in zip(banks[3:], pieces[3:])]
+        pieces = [(t, cols) for cols in halves for t in range(2)] + [(t, cols) for t in range(2, PACK) for cols in halves]
+        tags = ["bank%d" % b for b in range(6)] + ["kn_turned", "kn_spread"]
+        banks = [ps.tile([P, HALF], F32, name="bank%d" % b, tag=tags[b]) for b in range(len(pieces))]
+        products = [(banks[0][:, cols], 0, cols) for cols in (slice(0, P), slice(P, HALF))]
+        products += [(bank[:], t, cols) for bank, (t, cols) in zip(banks[1:], pieces[1:])]
         for out, t, cols in products:
             nc.tensor.matmul_mx(
                 out=out,
@@ -149,9 +149,11 @@ def tile_attend_plq_assign_topk_kernel(tc, qT, k_words, k_scales, kn, qn, offs, 
         clamp(nc.vector, HALF, N)
         clamp(nc.gpsimd, N + HALF, 2 * N)
         cross(4)
-        clamp(nc.gpsimd, 2 * N, 2 * N + SHARE)
+        clamp(nc.gpsimd, 2 * N, 2 * N + HALF)
         cross(5)
-        clamp(nc.vector, 2 * N + SHARE, 3 * N)
+        cross(6)
+        cross(7)
+        clamp(nc.vector, 2 * N + HALF, 3 * N)
         clamp(nc.vector, 3 * N, PACK * N)
         square_on_scalar(0, HALF)
         square_on_scalar(N, N + HALF)
@@ -167,11 +169,13 @@ def tile_attend_plq_assign_topk_kernel(tc, qT, k_words, k_scales, kn, qn, offs, 
         weights(3)
         nc.vector.reciprocal(inv[1][:], total[1][:])
         normed(0)
-        normed(1)
         nc.vector.reciprocal(inv[2][:], total[2][:])
+        normed(1)
         last = PACK - 1
         nc.vector.reciprocal(inv[last][:], total[last][:])
-        normed(2)
+        nc.scalar.activation(y[:, 2, 0:HELP], wt[2][:, 0:HELP], ACT.Copy, scale=inv[2][:])
+        nc.vector.tensor_scalar(y[:, 2, HELP:N], wt[2][:, HELP:N], inv[2][:], None, ALU.mult)
+        nc.sync.dma_start(out=out_rows[:, 2, :], in_=y[:, 2, :])
         for cols in (slice(0, P), slice(N - LAST, N)):
             nc.scalar.activation(y[:, last, cols], wt[last][:, cols], ACT.Copy, scale=inv[last][:])
         nc.vector.tensor_scalar(y[:, last, P : N - LAST], wt[last][:, P : N - LAST], inv[last][:], None, ALU.mult)

@@ -92,14 +92,16 @@ def tile_attend_plq_assign_topk_kernel(tc, qT, k_words, k_scales, kn, qn, offs, 
 
         k_code = sb.tile([P, N], U32, name="k_code", align_bytes=64)
         halves = [slice(0, HALF), slice(HALF, N)]
-        for first, last in ((0, P), (P, HALF), (HALF, N)):
+        for first, last in [(j * P, (j + 1) * P) for j in range(PACK)]:
             nc.vector.tensor_copy(k_code[:, first:last], word_pool[:].bitcast(U32).indirect(offsets[:, first // 16 : last // 16]))
 
         pieces = [(t, cols) for cols in halves for t in range(2)] + [(t, cols) for t in range(2, PACK) for cols in halves]
         tags = ["bank%d" % b for b in range(6)] + ["kn_turned", "kn_spread"]
         banks = [ps.tile([P, HALF], F32, name="bank%d" % b, tag=tags[b]) for b in range(len(pieces))]
         products = [(banks[0][:, cols], 0, cols) for cols in (slice(0, P), slice(P, HALF))]
-        products += [(bank[:], t, cols) for bank, (t, cols) in zip(banks[1:], pieces[1:])]
+        products += [(banks[1][:], 1, halves[0])]
+        products += [(banks[2][:, j * P : (j + 1) * P], 0, slice(HALF + j * P, HALF + (j + 1) * P)) for j in range(2)]
+        products += [(bank[:], t, cols) for bank, (t, cols) in zip(banks[3:], pieces[3:])]
         for out, t, cols in products:
             nc.tensor.matmul_mx(
                 out=out,

@@ -20,12 +20,12 @@ P = 128
 PACK = 4
 HALF = N // 2
 Q_SPLIT = 52
-LOWEST = -(2.0 ** 80)
+LOWEST = -(2.0 ** 79)
 ROWS = 16
 LAST = 96
-SHARE = 192
+SHARE = 128
 HELP = 128
-SHRINK = 2.0 ** -17
+SHRINK = 2.0 ** -16
 
 
 def tile_attend_plq_assign_topk_kernel(tc, qT, k_words, k_scales, kn, qn, offs, out_0, out_1, out_2):
@@ -79,13 +79,15 @@ def tile_attend_plq_assign_topk_kernel(tc, qT, k_words, k_scales, kn, qn, offs, 
         for j in range(PACK):
             nc.tensor.transpose(kn_spread[:, j * P : (j + 1) * P], kn_cols[:, j : j + 1].to_broadcast([P, P]), ident[:])
         kn_all = sb.tile([P, N], F32, name="kn_all")
-        nc.scalar.activation(kn_all[:], kn_spread[:], ACT.Copy, bias=1.0)
+        nc.scalar.activation(kn_all[:], kn_spread[:], ACT.Copy, scale=0.5)
+        qn_half = sb.tile([P, PACK], F32, name="qn_half")
+        nc.scalar.activation(qn_half[:], qn_cols[:], ACT.Copy, scale=0.5, bias=0.5)
 
         q_bf = sb.tile([P, PACK, P, PACK], BF16, name="q_bf", align_bytes=64)
         q_dst = q_bf[:].rearrange("p t m j -> p m j t")
         q_src = q_raw[:].rearrange("p j (m t) -> p m j t", t=PACK)
-        nc.scalar.activation(q_dst[:, 0:Q_SPLIT], q_src[:, 0:Q_SPLIT], ACT.Copy, scale=2.0)
-        nc.vector.tensor_scalar(q_dst[:, Q_SPLIT:P], q_src[:, Q_SPLIT:P], 2.0, None, ALU.mult)
+        nc.scalar.copy(q_dst[:, 0:Q_SPLIT], q_src[:, 0:Q_SPLIT])
+        nc.vector.tensor_copy(q_dst[:, Q_SPLIT:P], q_src[:, Q_SPLIT:P])
         q_code = sb.tile([P, NQ], U32, name="q_code", align_bytes=64)
         q_scale = sb.tile([P, NQ], U8, name="q_scale", align_bytes=64)
         nc.vector.quantize_mx(out=q_code[:].bitcast(FP8X4), scales=q_scale[:], in_=q_bf[:].rearrange("p t m j -> p (t m j)"))
@@ -124,10 +126,10 @@ def tile_attend_plq_assign_topk_kernel(tc, qT, k_words, k_scales, kn, qn, offs, 
 
         def cross(b):
             t, cols = pieces[b]
-            nc.vector.scalar_tensor_tensor(dist[t][:, cols], banks[b][:], qn_cols[:, t : t + 1], kn_all[:, cols], ALU.subtract, ALU.subtract)
+            nc.vector.scalar_tensor_tensor(dist[t][:, cols], banks[b][:], qn_half[:, t : t + 1], kn_all[:, cols], ALU.subtract, ALU.subtract)
 
         def clamp(engine, first, last):
-            engine.tensor_scalar(dist_all[:, first:last], dist_all[:, first:last], -1.0, LOWEST, ALU.min, ALU.max)
+            engine.tensor_scalar(dist_all[:, first:last], dist_all[:, first:last], -0.5, LOWEST, ALU.min, ALU.max)
 
         def square_on_scalar(first, last):
             nc.scalar.activation(sq_all[:, first:last], dist_all[:, first:last], ACT.Square, scale=SHRINK)

from contextlib import ExitStack

import concourse.mybir as mybir
from concourse.masks import make_identity

D, NQ, T, N = 512, 512, 2048, 512
FLOPS = 2 * D * NQ * N

F32 = mybir.dt.float32
BF16 = mybir.dt.bfloat16
I32 = mybir.dt.int32
U32 = mybir.dt.uint32
U16 = mybir.dt.uint16
U8 = mybir.dt.uint8
FP8X4 = mybir.dt.float8_e4m3fn_x4
ALU = mybir.AluOpType
ACT = mybir.ActivationFunctionType

P = 128
PACK = 4
HALF = N // 2
Q_SPLIT = 52
LOWEST = -(2.0 ** 79)
ROWS = 16
LAST = 96
SHARE = 128
HELP = 128
SHRINK = 2.0 ** -16


def tile_attend_plq_assign_topk_kernel(tc, qT, k_words, k_scales, kn, qn, offs, out_0, out_1, out_2):
    nc = tc.nc
    with ExitStack() as ctx:
        sb = ctx.enter_context(tc.tile_pool(name="sb", bufs=1))
        ps = ctx.enter_context(tc.psum_pool(name="ps", bufs=1))

        offsets = sb.tile([P, N // 16], U16, name="offsets")
        nc.sync.dma_start(offsets[:], offs)

        one = sb.tile([P, 1], F32, name="one")
        nc.vector.memset(one[:], 1.0)
        scale_pool = sb.tile([P, T], U8, name="scale_pool")
        nc.sync.dma_start(out=scale_pool[P - ROWS : P, :].bitcast(I32), in_=k_scales[0].bitcast(I32))
        nc.gpsimd.memset(scale_pool[0 : P - ROWS, :].bitcast(I32), 0)
        kn_pool = sb.tile([P, T], F32, name="kn_pool")
        nc.sync.dma_start(out=kn_pool[P - 1 : P, :], in_=kn[0:1, :])
        nc.vector.memset(kn_pool[0 : P - 1, :], 0.0)

        q_raw = sb.tile([P, PACK, NQ], F32, name="q_raw")
        nc.sync.dma_start(out=q_raw[:], in_=qT[0].rearrange("(p j) q -> p j q", j=PACK))
        word_pool = sb.tile([P, T], I32, name="word_pool")
        nc.sync.dma_start(out=word_pool[:], in_=k_words[0].rearrange("p t r -> p (t r)").bitcast(I32))


        ident = sb.tile([P, P], F32, name="ident")
        make_identity(nc, ident[:])
        warm = sb.tile([P, 1], F32, name="warm")
        nc.scalar.activation(warm[:], one[:], ACT.Abs_reciprocal_sqrt, bias=one[:])

        picked = sb.tile([P, N], U8, name="picked")
        nc.vector.tensor_copy(picked[:], scale_pool[:].indirect(offsets[:]))
        k_scale = sb.tile([P, N], U8, name="k_scale", align_bytes=64)
        nc.gpsimd.memset(k_scale[:].bitcast(I32), 0)
        for quad in range(4):
            first = P - ROWS + 4 * quad
            nc.sync.dma_start(out=k_scale[32 * quad : 32 * quad + 4, :].bitcast(I32), in_=picked[first : first + 4, :].bitcast(I32))

        qn_cols = sb.tile([P, PACK], F32, name="qn_cols", tag="scale_pool")
        nc.sync.dma_start(out=qn_cols[:], in_=qn[0].rearrange("(p t) o -> p (t o)", t=PACK))

        kn_row = sb.tile([P, N], F32, name="kn_row")
        nc.scalar.activation(kn_row[:], kn_pool[:].indirect(offsets[:]), ACT.Copy)
        kn_turned = ps.tile([P, PACK, P], F32, name="kn_turned")
        for j in range(PACK):
            nc.tensor.transpose(kn_turned[:, j, :], kn_row[:, j * P : (j + 1) * P], ident[:])
        kn_cols = sb.tile([P, PACK], F32, name="kn_cols")
        nc.scalar.copy(kn_cols[:], kn_turned[:, :, P - 1])
        kn_spread = ps.tile([P, N], F32, name="kn_spread")
        for j in range(PACK):
            nc.tensor.transpose(kn_spread[:, j * P : (j + 1) * P], kn_cols[:, j : j + 1].to_broadcast([P, P]), ident[:])
        kn_all = sb.tile([P, N], F32, name="kn_all")
        nc.scalar.activation(kn_all[:], kn_spread[:], ACT.Copy, scale=0.5)
        qn_half = sb.tile([P, PACK], F32, name="qn_half")
        nc.scalar.activation(qn_half[:], qn_cols[:], ACT.Copy, scale=0.5, bias=0.5)

        q_bf = sb.tile([P, PACK, P, PACK], BF16, name="q_bf", align_bytes=64)
        q_dst = q_bf[:].rearrange("p t m j -> p m j t")
        q_src = q_raw[:].rearrange("p j (m t) -> p m j t", t=PACK)
        nc.scalar.copy(q_dst[:, 0:Q_SPLIT], q_src[:, 0:Q_SPLIT])
        nc.vector.tensor_copy(q_dst[:, Q_SPLIT:P], q_src[:, Q_SPLIT:P])
        q_code = sb.tile([P, NQ], U32, name="q_code", align_bytes=64)
        q_scale = sb.tile([P, NQ], U8, name="q_scale", align_bytes=64)
        nc.vector.quantize_mx(out=q_code[:].bitcast(FP8X4), scales=q_scale[:], in_=q_bf[:].rearrange("p t m j -> p (t m j)"))

        k_code = sb.tile([P, N], U32, name="k_code", align_bytes=64)
        halves = [slice(0, HALF), slice(HALF, N)]
        for first, last in [(j * P, (j + 1) * P) for j in range(PACK)]:
            nc.vector.tensor_copy(k_code[:, first:last], word_pool[:].bitcast(U32).indirect(offsets[:, first // 16 : last // 16]))

        pieces = [(t, cols) for cols in halves for t in range(2)] + [(t, cols) for t in range(2, PACK) for cols in halves]
        tags = ["bank%d" % b for b in range(6)] + ["kn_turned", "kn_spread"]
        banks = [ps.tile([P, HALF], F32, name="bank%d" % b, tag=tags[b]) for b in range(len(pieces))]
        products = [(banks[0][:, cols], 0, cols) for cols in (slice(0, P), slice(P, HALF))]
        products += [(banks[1][:], 1, halves[0])]
        products += [(banks[2][:, j * P : (j + 1) * P], 0, slice(HALF + j * P, HALF + (j + 1) * P)) for j in range(2)]
        products += [(bank[:], t, cols) for bank, (t, cols) in zip(banks[3:], pieces[3:])]
        for out, t, cols in products:
            nc.tensor.matmul_mx(
                out=out,
                lhsT=q_code[:, t * P : (t + 1) * P].bitcast(FP8X4),
                lhsT_scale=q_scale[:, t * P : (t + 1) * P],
                rhs=k_code[:, cols].bitcast(FP8X4),
                rhs_scale=k_scale[:, cols],
                start=True,
                stop=True,
            )

        y = sb.tile([P, PACK, N], F32, name="y")
        out_rows = out_0.rearrange("(p t) i -> p t i", t=PACK)
        dist_all = sb.tile([P, PACK * N], F32, name="dist_all")
        dist = [dist_all[:, t * N : (t + 1) * N] for t in range(PACK)]
        sq_all = sb.tile([P, PACK * N], F32, name="sq_all")
        wt = [sb.tile([P, N], F32, name="wt%d" % t) for t in range(PACK)]
        total = [sb.tile([P, 1], F32, name="total%d" % t) for t in range(PACK)]
        inv = [sb.tile([P, 1], F32, name="inv%d" % t) for t in range(PACK)]

        def cross(b):
            t, cols = pieces[b]
            nc.vector.scalar_tensor_tensor(dist[t][:, cols], banks[b][:], qn_half[:, t : t + 1], kn_all[:, cols], ALU.subtract, ALU.subtract)

        def clamp(engine, first, last):
            engine.tensor_scalar(dist_all[:, first:last], dist_all[:, first:last], -0.5, LOWEST, ALU.min, ALU.max)

        def square_on_scalar(first, last):
            nc.scalar.activation(sq_all[:, first:last], dist_all[:, first:last], ACT.Square, scale=SHRINK)

        def square_on_vector(first, last):
            nc.vector.scalar_tensor_tensor(sq_all[:, first:last], dist_all[:, first:last], SHRINK * SHRINK, dist_all[:, first:last], ALU.mult, ALU.mult)

        def weights(t):
            nc.scalar.activation(wt[t][:], sq_all[:, t * N : (t + 1) * N], ACT.Abs_reciprocal_sqrt, accum_out=total[t][:])

        def normed(t):
            nc.vector.tensor_scalar(y[:, t, :], wt[t][:], inv[t][:], None, ALU.mult)
            nc.sync.dma_start(out=out_rows[:, t, :], in_=y[:, t, :])

        cross(0)
        cross(1)
        clamp(nc.vector, 0, HALF)
        clamp(nc.gpsimd, N, N + HALF)
        cross(2)
        cross(3)
        clamp(nc.vector, HALF, N)
        clamp(nc.gpsimd, N + HALF, 2 * N)
        cross(4)
        clamp(nc.gpsimd, 2 * N, 2 * N + HALF)
        cross(5)
        cross(6)
        cross(7)
        clamp(nc.vector, 2 * N + HALF, 3 * N)
        clamp(nc.vector, 3 * N, PACK * N)
        square_on_scalar(0, HALF)
        square_on_scalar(N, N + HALF)
        square_on_scalar(HALF, N)
        square_on_scalar(N + HALF, 2 * N)
        weights(0)
        square_on_scalar(2 * N, 2 * N + SHARE)
        weights(1)
        square_on_vector(2 * N + SHARE, 3 * N)
        nc.vector.reciprocal(inv[0][:], total[0][:])
        square_on_vector(3 * N, PACK * N)
        weights(2)
        weights(3)
        nc.vector.reciprocal(inv[1][:], total[1][:])
        normed(0)
        nc.vector.reciprocal(inv[2][:], total[2][:])
        normed(1)
        last = PACK - 1
        nc.vector.reciprocal(inv[last][:], total[last][:])
        nc.scalar.activation(y[:, 2, 0:HELP], wt[2][:, 0:HELP], ACT.Copy, scale=inv[2][:])
        nc.vector.tensor_scalar(y[:, 2, HELP:N], wt[2][:, HELP:N], inv[2][:], None, ALU.mult)
        nc.sync.dma_start(out=out_rows[:, 2, :], in_=y[:, 2, :])
        for cols in (slice(0, P), slice(N - LAST, N)):
            nc.scalar.activation(y[:, last, cols], wt[last][:, cols], ACT.Copy, scale=inv[last][:])
        nc.vector.tensor_scalar(y[:, last, P : N - LAST], wt[last][:, P : N - LAST], inv[last][:], None, ALU.mult)
        nc.sync.dma_start(out=out_rows[:, last, :], in_=y[:, last, :])

        y_code = sb.tile([P, N], U32, name="y_code", align_bytes=64)
        y_scale = sb.tile([P, N], U8, name="y_scale", align_bytes=64)
        out_words = out_1[0].rearrange("p i u -> p (i u)").bitcast(I32)
        y_bf = sb.tile([P, N, PACK], BF16, name="y_bf", align_bytes=64)
        for copy, cols in ((nc.scalar.copy, slice(0, P)), (nc.vector.tensor_copy, slice(P, N - LAST)), (nc.scalar.copy, slice(N - LAST, N))):
            copy(y_bf[:, cols, :].rearrange("p (c i) t -> p c t i", i=4), y[:, :, cols].rearrange("p t (c i) -> p c t i", i=4))
        for cols in (slice(0, P), slice(P, 3 * P), slice(3 * P, N)):
            nc.vector.quantize_mx(out=y_code[:, cols].bitcast(FP8X4), scales=y_scale[:, cols], in_=y_bf[:, cols, :].rearrange("p i t -> p (i t)"))
        for cols in (slice(0, 3 * P), slice(3 * P, N)):
            nc.sync.dma_start(out=out_words[:, cols], in_=y_code[:, cols].bitcast(I32))
        for r in range(4):
            nc.sync.dma_start(out=out_2[0, r:16:4, :].bitcast(I32), in_=y_scale[r:P:32, :].bitcast(I32))
